import numpy as np, ml_dtypes
CORES = [8,136,40,168]
N = 4
BF = ml_dtypes.bfloat16
P, M, C, I, D, S, SH = 256, 192, 512, 8, 1, 3, 7
J = I // D; U = 1 << SH; FILL = (P - M) // S + 2
def at(rng, t, e):
    b = e >> 4
    a = b + (((np.arange(16)[:, None] + rng.integers(0, 16, e.shape)) & 15) < (e & 15))
    sh = e.shape[:-2] + (8, e.shape[-1])
    z = np.floor((np.minimum(b, 127 - b) + 1) * rng.random(sh)).astype(np.int64) * (2 * rng.integers(0, 2, sh) - 1)
    a[..., 0::2, :] += z; a[..., 1::2, :] -= z
    return t + np.where(t < 128, 1, -1) * a
def lean(rng, t, e, m):
    a = (e >> 4) + (((np.arange(16)[:, None] + rng.integers(0, 16, e.shape)) & 15) < (e & 15))
    z = rng.integers(0, m + 1, e.shape[:-2] + (8, e.shape[-1]))
    a[..., 0::2, :] -= z; a[..., 1::2, :] += z
    return t + a
def far(rng, t, k):
    u = rng.integers(0, 16, t.shape[:-1] + (k,))
    return np.where(t < 128, 255 - u, u)
def parts(rng, dev):
    t = np.clip(rng.integers(0, 256, (1, 8, 16, 1)) + rng.integers(-dev, dev + 1, (N, 8, 16, 1)), 0, 255)
    e = U * np.repeat(np.arange(16), M) + rng.integers(0, U, (N, 8, 1, 16 * M))
    return {"t": t, "n": rng.integers(M >> 1, M + 1, (N, 8, 16)), "hs": at(rng, t, e), "x": at(rng, t, rng.integers(0, 16 * U, (N, 8, 1, C))),
            "dv": rng.integers(0, 256, (N, 8, 16, S * C)) >> rng.integers(0, 8, (N, 8, 1, S * C)), "te": rng.integers(0, 5, (N, 8))}
def pack(p):
    def b(v):
        return np.ascontiguousarray(v.reshape(N, 128, -1)).astype(np.float32).astype(BF)
    return {"hs": b(p["hs"]), "cn": p["n"].reshape(N, 128, 1).astype(np.int32), "x0": b(p["x"]), "tg": b(p["t"]), "dv": b(p["dv"]),
            "te": np.repeat(p["te"], 16, axis=1).reshape(N, 128, 1).astype(np.int32)}
def setup_inputs(rng):
    p = parts(rng, 4); t = p["t"]
    lo = rng.integers(0, 12, (N, 8, 1, 1)); wd = rng.choice(np.array([1, 4, 16]), (N, 8, 1, 1))
    e = np.minimum((lo * U + wd * U * rng.random((N, 8, 1, C))).astype(np.int64), 16 * U - 1)
    low = np.zeros((N, 8, 1, 1), bool); low[np.arange(N), rng.integers(0, 8, N)] = True
    e = np.where(low, rng.integers(0, U, e.shape), e); p["te"] = np.where(low[..., 0, 0], 0, p["te"])
    away = (rng.random(e.shape) < 0.125) & ~low
    p["x"] = np.where(away, far(rng, t, C), at(rng, t, e))
    p["hs"][..., 15 * M:] = np.where(rng.random((N, 8, 1, M)) < 0.25, far(rng, t, M), p["hs"][..., 15 * M:])
    return pack(p)
def setup_inputs_caps(rng):
    p = parts(rng, 0); p["te"] = 0 * p["te"]; p["dv"] = 0 * p["dv"]; kr = np.zeros((N, 8, 1, C), np.int64); ov = rng.integers(0, 15, 8)
    F = min(C, P >> 1); fk = rng.integers(3, 8, 8)
    for g in (2, 3):
        k = int(fk[g])
        goal = 2655 - ((97 * (I - 1) + 5 * (C - 1) + U) >> 1) - U * k
        p["t"][:, g] = at(rng, np.zeros((16, 1), np.int64), np.array([[goal]]))
        p["hs"][:, g] = at(rng, p["t"][:, g], U * np.repeat(np.arange(16), M) + rng.integers(0, U, (N, 1, 16 * M)))
        p["hs"][:, g, :, k * M:(k + 1) * M] = lean(rng, p["t"][:, g], U * k + rng.integers(1, U, (N, 1, M)), U * k >> 5)
    for r in range(N):
        for g in range(8):
            if g < 2:
                o = rng.permutation(16)
                kr[r, g, 0] = rng.permutation(np.concatenate([np.repeat(o[:3], FILL), rng.choice(o[3:9], C - 3 * FILL)]))
                p["n"][r, g, o[:3]] = P + np.array([0, -1, 1]) - S * FILL
            elif g < 4:
                k = int(fk[g])
                kr[r, g, 0] = rng.choice(np.delete(np.arange(16), k), C)
                kr[r, g, 0, rng.permutation(C)[:F]] = k
                p["n"][r, g, k] = P - F
            else:
                k = int(ov[g])
                kr[r, g, 0] = rng.permutation(np.concatenate([np.repeat(k, C - 4), np.repeat(k + 1, 4)]))
                p["n"][r, g, k] = M; p["n"][r, g, k + 1] = 1
    p["x"] = at(rng, p["t"], U * kr + rng.integers(0, U, kr.shape))
    for r in range(N):
        for g in (2, 3):
            k = int(fk[g]); c = np.flatnonzero(kr[r, g, 0] == k)
            p["x"][r, g][:, c] = lean(rng, p["t"][r, g], U * k + rng.integers(1, U, (1, len(c))), U * k >> 5)
            p["x"][r, g, :, int(c[-1])] = p["t"][r, g, :, 0] + (U * k >> 3) * (1 - (np.arange(16) & 1))
    return pack(p)
def setup_inputs_crowd(rng):
    p = parts(rng, 4); kr = rng.integers(0, 16, (N, 8, 1, 1)); kr[:, 0] = 0; kr[:, 1] = 15; kr[:, 2] = 15
    p["x"] = at(rng, p["t"], U * kr + rng.integers(0, U, (N, 8, 1, C)))
    p["n"] = np.where(np.arange(16) == kr[..., 0], M, p["n"])
    p["te"] = rng.choice(np.array([0, 0, 3, 1024]), (N, 8))
    t = 255 * rng.integers(0, 2, (N, 16, 1)); p["t"][:, 2] = t
    p["hs"][:, 2] = at(rng, t, U * np.repeat(np.arange(16), M) + rng.integers(0, U, (N, 1, 16 * M)))
    p["hs"][:, 2, :, 15 * M:] = far(rng, t, M)
    p["x"][:, 2] = np.where(np.arange(C) & 1, far(rng, t, C), 255 - t)
    return pack(p)
def setup_inputs_ties(rng):
    p = parts(rng, 0); t = p["t"]; lv = np.array([0, U >> 2, U >> 1, U - 1])
    p["hs"] = at(rng, t, U * np.repeat(np.arange(16), M) + rng.choice(lv, (N, 8, 1, 16 * M)))
    x = at(rng, t, U * rng.integers(0, 16, (N, 8, 1, C)) + rng.choice(lv, (N, 8, 1, C)))
    on = (rng.random((N, 8, 1, C)) < 0.5) & (np.arange(8)[:, None, None] >= 4)
    p["x"] = np.where(on, t, x); p["te"] = rng.integers(0, 9, (N, 8)); p["te"][:, :2] = 0
    p["dv"] = p["dv"] * rng.integers(0, 2, (N, 8, 1, S * C))
    back = np.where(t < 128, np.clip(2 * (p["x"] - t), 0, 255), 0)
    p["dv"][..., :C] = np.where(rng.random((N, 8, 1, C)) < 0.7, back, p["dv"][..., :C])
    y = rng.integers(240, 256, (16, 1)); y[0, 0] ^= int(np.add.reduce(y[:, 0])) & 1
    u = rng.integers(32, 41, (16, 1)); ty = int(np.add.reduce(y[:, 0])); tu = int(np.add.reduce(u[:, 0]))
    p["t"][:, 3] = u; p["hs"][:, 3] = y; p["dv"][:, 3] = 0
    for r in range(N):
        T, m = ((257, 8), (513, 4), (1021, 3), (1024, 2))[r & 3]
        e = ty - tu - T * m; v = ((tu + e - m) & 63) >> 1
        b = (e - v) // 15
        a = b + (((np.arange(15)[:, None] + rng.integers(0, 15, (1, C))) % 15) < e - v - 15 * b)
        z = rng.integers(0, b + 1, (7, C)) * (2 * rng.integers(0, 2, (7, C)) - 1)
        a[0:14:2] += z; a[1:14:2] -= z
        p["x"][r, 3] = np.concatenate([u[:15] + a, np.full((1, C), int(u[15, 0]) - v)], axis=0); p["te"][r, 3] = T
    return pack(p)
def setup_inputs_alike(rng):
    p = parts(rng, 4)
    p["x"] = np.repeat(at(rng, p["t"], rng.integers(0, 16 * U, (N, 8, 1, 1))), C, axis=3)
    p["n"] = rng.choice(np.array([1, 2, 3, M]), (N, 8, 16))
    p["hs"] = p["hs"][..., np.arange(16 * M) >> 2 << 2]
    return pack(p)
def setup_inputs_spread(rng):
    def un(*sh):
        return np.floor(np.exp2(8 * rng.random(sh[:-2] + (1, sh[-1]))) * rng.random(sh)).astype(np.int64)
    p = {"t": rng.integers(0, 256, (N, 8, 16, 1)), "hs": un(N, 8, 16, 16 * M), "x": un(N, 8, 16, C), "dv": un(N, 8, 16, S * C)}
    p["n"] = 1 + np.floor(M * rng.random((N, 8, 16)) ** 3).astype(np.int64)
    p["te"] = np.floor(np.exp2(10 * rng.random((N, 8)))).astype(np.int64) * (rng.random((N, 8)) < 0.75)
    return pack(p)
def check_inputs(d):
    bad = []
    for k, lo, hi in (("hs", 0, 255), ("cn", 1, M), ("x0", 0, 255), ("tg", 0, 255), ("dv", 0, 255), ("te", 0, 1024)):
        v = np.asarray(d[k]).astype(np.float64)
        if not (np.all(v >= lo) and np.all(v <= hi) and np.all(v == np.floor(v))): bad.append("whole numbers and range of " + k)
    v = np.asarray(d["te"]).reshape(N, 8, 16)
    if not np.all(v == v[:, :, :1]): bad.append("te alike in a group")
    return bad
def num(a, k):
    return a.astype(np.float32).astype(np.int64).reshape(N, 8, 16, k)
def energy(z, t):
    return np.add.reduce(np.abs(z - t), axis=-2)
def reference(hs, cn, x0, tg, dv, te):
    x = num(x0, C); goal = num(tg, 1); mv = num(dv, S * C); n = cn.astype(np.int64).reshape(N, 8, 16); T = te.astype(np.int64).reshape(N, 8, 16)[:, :, :1]
    H = np.zeros((N, 8, 16, 16, P), np.int64); H[..., :M] = num(hs, 16 * M).reshape(N, 8, 16, 16, M); H = H.reshape(N, 8, 16, 16 * P)
    cs = np.arange(C)
    for t in range(S):
        E = energy(x, goal); k = np.minimum(15, E >> SH); s = np.add.reduce(x, axis=2)
        bound = E + T * (s & 63); new = []
        for r in range(N):
            ys = []
            for d in range(D):
                q = (r + 1 + d) % N; i = d * J + np.arange(J)
                w = (s[r][:, None, :] + 97 * i[None, :, None] + 31 * t + 5 * cs) & 4095
                h = ((w * w >> 7) + w) & 4095
                nk = np.take_along_axis(n[q], k[r], 1)
                col = P * k[r][:, None, :] + (h * nk[:, None, :] >> 12)
                ys.append(np.take_along_axis(H[q], col.reshape(8, 1, J * C), 2).reshape(8, 16, J, C))
            ys = np.concatenate(ys, axis=2)
            dist = np.add.reduce(np.abs(ys - x[r][:, :, None, :]), axis=1)
            best = np.argmax(dist, axis=1)
            y = np.take_along_axis(ys, best[:, None, None, :], 2)[:, :, 0, :]
            z = np.abs(x[r] - mv[r][..., t * C:(t + 1) * C])
            oky = energy(y, goal[r]) <= bound[r]; okz = energy(z, goal[r]) <= bound[r]
            new.append(np.where(oky[:, None, :], y, np.where(okz[:, None, :], z, x[r])))
        x = np.stack(new)
        k = np.minimum(15, energy(x, goal) >> SH)
        eq = (k[:, :, None, :] == np.arange(16)[:, None]).astype(np.int64)
        place = np.take_along_axis(n[..., None] + np.add.accumulate(eq, axis=3) - eq, k[:, :, None, :], 2)[:, :, 0, :]
        for r in range(N):
            for g in range(8):
                m = place[r, g] < P
                H[r, g][:, (P * k[r, g] + place[r, g])[m]] = x[r, g][:, m]
        n = np.minimum(P, n + np.add.reduce(eq, axis=3))
    return {"yx": x.reshape(N, 128, C).astype(np.float32).astype(BF), "yn": n.reshape(N, 128, 1).astype(np.float32)}

@@ -1,0 +1,413 @@
+from concourse.mybir import AluOpType as A, ActivationFunctionType as F
+
+C, NT, NS, M = 512, 8, 3, 192
+HB = 3 * 1536
+XO = [2 * 1536, 1536, 0]
+CH = [(0, 4), (4, 11), (11, 16)]
+BF, F32, I32, U16, F16 = "bfloat16", "float32", "int32", "uint16", "float16"
+
+SBUF = {
+    BF: {"W": HB + 12288, "hsb": 8 + 3072, "hsl": 8 + 3072, "mv": 1536, "xout": 512, "d": 4096, "ad": 4096, "yb": 1024,
+         "eq": 512, "tgb": 16, "ident": 128, "nident": 128, "zero": 128, "id16": 16,
+         "z1": 144, "zd": 144, "zm": 144, "zy": 144, "zn": 144, "ce": 64, "tie": 256, "kb": 32,
+         "xl1": 512, "xl2": 512},
+    F32: {"col": 16, "ixf": 128, "cts": 768, "cj": 32, "ck": 192, "mk": 64, "eo": 64, "so": 64, "co": 64,
+          "ef": 64, "sf": 64, "cf": 64, "tm": 32, "bnd": 32, "prod": 256, "run": 64, "run2": 64, "wc": 32, "cnt": 8,
+          "n0": 8, "n1": 8, "n2": 8, "n3": 8, "nl1": 8, "nl2": 8},
+    I32: {"tei": 8, "cni": 8, "ia": 128, "ib": 32, "ct": 256, "ki": 32, "si": 32, "sm": 32, "w0": 256, "w": 256, "pw": 256,
+          "h": 256, "best": 32, "wp": 32},
+    U16: {"bc": 16, "k16": 32, "c16": 32, "w16": 32, "off": 256, "os1": 32, "os2": 32, "ol1": 32, "ol2": 32},
+    F16: {"plh": 256, "i16h": 128, "z16h": 144, "u": 512, "m": 512},
+}
+SCRATCH = {name: ("sbuf", [128, n], dt) for dt, bufs in SBUF.items() for name, n in bufs.items()}
+SCRATCH.update({name: ("psum", [128, 512], F32) for name in ("pka", "pkb", "pes", "pzw", "pze", "po", "pp", "pw2")})
+LOADS = ["lh%d" % k for k in range(len(CH))] + ["lcn", "lx", "ly", "ltg", "lte", "lmv", "sx", "sn"]
+ARRIVE = ["ah%d" % k for k in range(len(CH))] + ["an1", "an2", "ax1", "ax2", "ao1", "ao2"]
+SEMAPHORES = ["qv", "qs", "qp", "qg", "sent"] + LOADS + ARRIVE
+
+
+def R(name, lo=0, hi=None, step=1):
+    return (name, lo, SCRATCH[name][1][1] if hi is None else hi, step)
+
+
+def rank_program(g, core, T, topo):
+    rank = T.rank_of(core)
+    if rank is None:
+        return
+    n_ranks = len(T.cores)
+    dst = T.cores[(rank - 1) % n_ranks]
+    src = T.cores[(rank + 1) % n_ranks]
+    rid, pid = topo.addr(dst, core)
+    mask = topo.mask(core, dst)
+    n_out, n_in = len(topo.engines(core, dst)), len(topo.engines(src, core))
+    Q = {"v": g.vector, "s": g.scalar, "p": g.tensor, "g": g, "y": g.sync}
+    count = {"qv": 0, "qs": 0, "qp": 0, "qg": 0, "sent": 0}
+    known = {q: {} for q in Q}
+    log = {name: [] for name in SCRATCH}
+
+    def ap(r):
+        return T[r[0]][:, r[1]:r[2]:r[3]] if r[3] != 1 else T[r[0]][:, r[1]:r[2]]
+
+    def cols(r):
+        return set(range(512)) if SCRATCH[r[0]][0] == "psum" else set(range(r[1], r[2], r[3]))
+
+    def order(q, reads, writes):
+        need = {}
+        for rs, wr in ((reads, False), (writes, True)):
+            for r in rs:
+                cs, psum = cols(r), SCRATCH[r[0]][0] == "psum"
+                for (c2, w2, q2, sem, val, clock) in log[r[0]]:
+                    if q == "p" and q2 == "p":
+                        continue
+                    if (wr or w2 or (psum and q2 != q)) and known[q].get(sem, 0) < val and not cs.isdisjoint(c2):
+                        if val > need.get(sem, (0, None))[0]:
+                            need[sem] = (val, clock)
+        for sem, (val, clock) in sorted(need.items(), key=lambda e: -sum(e[1][1].values())):
+            if known[q].get(sem, 0) < val:
+                Q[q].wait_ge(T.sem[sem], val)
+                known[q][sem] = val
+                for s2, v2 in clock.items():
+                    known[q][s2] = max(known[q].get(s2, 0), v2)
+
+    def call(q, make, reads, writes):
+        order(q, reads, writes)
+        sem = "q" + q
+        count[sem] += 1
+        make().then_inc(T.sem[sem], 1)
+        clock = dict(known[q])
+        for r in writes:
+            cs = cols(r)
+            log[r[0]][:] = [e for e in log[r[0]] if not e[0] <= cs]
+            log[r[0]].append((cs, True, q, sem, count[sem], clock))
+        for r in reads:
+            log[r[0]].append((cols(r), False, q, sem, count[sem], clock))
+
+    def opnd(x):
+        if not isinstance(x, tuple):
+            return x, [], []
+        if x[0] == "ind":
+            return ap(x[1]).indirect(ap(x[2])), [x[1]], [x[2]]
+        return ap(x), [x], []
+
+    def tt(out, a, b, op):
+        (o, wo, _), (x, rx, ox), (y, ry, _) = opnd(out), opnd(a), opnd(b)
+        call("v", lambda: g.vector.tensor_tensor(o, x, y, op), rx + ox + ry, wo)
+
+    def ts(out, a, s1, op0, s2=None, op1=None):
+        (o, wo, _), (x, rx, ox), (y, ry, _), (z, rz, _) = opnd(out), opnd(a), opnd(s1), opnd(s2)
+        if op1 is None:
+            call("v", lambda: g.vector.tensor_scalar(o, x, y, None, op0), rx + ox + ry, wo)
+        else:
+            call("v", lambda: g.vector.tensor_scalar(o, x, y, z, op0, op1), rx + ox + ry + rz, wo)
+
+    def cp(out, a):
+        (o, wo, oo), (x, rx, ox) = opnd(out), opnd(a)
+        call("v", lambda: g.vector.tensor_copy(o, x), rx + ox + oo, wo)
+
+    def fill(out, v):
+        call("v", lambda: g.vector.memset(ap(out), v), [], [out])
+
+    def scan(out, d0, d1, init, op0, op1):
+        x, rx, _ = opnd(init)
+        call("v", lambda: g.vector.tensor_tensor_scan(ap(out), ap(d0), ap(d1), x, op0, op1), [d0, d1] + rx, [out])
+
+    def act(out, a, func, bias=None, accum=None):
+        x, rx, ox = opnd(a)
+        kw = {}
+        if bias is not None:
+            kw["bias"] = ap(bias)
+        if accum is not None:
+            kw["accum_out"] = ap(accum)
+        call("s", lambda: g.scalar.activation(ap(out), x, func, **kw),
+             rx + ox + ([bias] if bias else []), [out] + ([accum] if accum else []))
+
+    def mm(out, lhs, rhs, start, stop):
+        call("p", lambda: g.tensor.matmul(ap(out), ap(lhs), ap(rhs), start, stop), [lhs, rhs], [out])
+
+    def compact(out, z, buf, lo, hi, start, stop):
+        for p in range(16):
+            mm(out, R(z, 15 - p, 143 - p), R(buf, lo + p, hi, 16), start and p == 0, stop and p == 15)
+
+    def load(q, sem, out, dram):
+        order(q, [], [out])
+        Q[q].dma_start(ap(out), dram).then_inc(T.sem[sem], 16)
+        log[out[0]].append((cols(out), True, "dma", sem, 16, dict(known[q])))
+
+    def store(q, sem, dram, a):
+        order(q, [a], [])
+        Q[q].dma_start(dram, ap(a)).then_inc(T.sem[sem], 16)
+
+    def send(a, land, sem):
+        order("g", [a], [])
+        g.remote_dma(ap(land), ap(a), T.sem[sem], T.sem.sent, pid, rid, mask)
+        count["sent"] += n_out
+        log[land[0]].append((cols(land), True, "dma", sem, n_in, {}))
+
+    def col(j):
+        return R("col", j, j + 1)
+
+    def odd(name):
+        return R(name, 1, 64, 2)
+
+    def even(name):
+        return R(name, 0, 64, 2)
+
+    def chunk(name, k, head=False):
+        return R(name, 0 if head else 8 + M * CH[k][0], 8 + M * CH[k][1])
+
+    HIST = R("W", HB, HB + 4096)
+
+    for k in range(len(CH)):
+        load("y", "lh%d" % k, chunk("hsb", k), T.hs[:, M * CH[k][0]:M * CH[k][1]])
+    load("s", "lcn", R("cni", 0, 1), T.cn[:])
+    load("s", "ly", R("yb", 0, C), T.x0[:])
+    load("s", "ltg", R("tgb", 0, 1), T.tg[:])
+    load("s", "lx", R("W", XO[0], XO[0] + C), T.x0[:])
+    load("y", "lte", R("tei", 0, 1), T.te[:])
+    load("y", "lmv", R("mv"), T.dv[:])
+
+    call("g", lambda: g.iota(ap(R("ia")), [[-1, 128]], 0, 1), [], [R("ia")])
+    call("g", lambda: g.iota(ap(R("ct")), [[97, NT], [80, 32]], 0, 0), [], [R("ct")])
+    call("g", lambda: g.iota(ap(R("tie")), [[-4096, NT], [0, 32]], 4096 * (NT - 1) - 20480, 0,
+                             allow_small_or_imprecise_dtypes=True), [], [R("tie")])
+    fill(R("hsb", 0, 8), 0.0)
+    fill(R("z1"), 0.0)
+    fill(R("ce", 0, 32), 0.0)
+    fill(R("ce", 32, 64), -63.5)
+    fill(R("mk"), 0.0)
+    fill(R("so"), 0.0)
+    fill(R("zero"), 0.0)
+    ts(R("ib", 0, 8), R("ia", 0, 128, 16), 4, A.arith_shift_right)
+    ts(R("ib", 8, 24), R("ia", 0, 16), 15, A.bitwise_and)
+    ts(R("ident"), R("ia"), 0.0, A.is_equal)
+    ts(R("z1", 15, 143, 16), R("ib", 0, 8), 0.0, A.is_equal)
+    ts(R("id16"), R("ib", 8, 24), 0.0, A.is_equal)
+    cp(col(2), R("ib", 8, 9))
+    ts(R("nident"), R("ia"), 0.0, A.is_equal, -1.0, A.mult)
+    ts(col(3), col(2), 5.0, A.mult)
+    ts(col(4), R("ia", 0, 1), 16.0, A.mult, col(2), A.add)
+    ts(R("i16h"), R("ia"), 0.0, A.is_equal, 16.0, A.mult)
+    ts(R("cj"), R("ia", 0, 32), -16.0, A.mult, col(4), A.add)
+    ts(R("zd"), R("z1"), 32768.0, A.mult)
+    ts(R("tm", 0, 2), R("cj", 0, 2), 2.0, A.mult, 1.0, A.add)
+    ts(R("cts", 0, 256), R("ct"), col(3), A.add)
+    cp(R("hsb", 7, 8), R("cni", 0, 1))
+    for k in range(len(CH)):
+        send(chunk("hsb", k, k == 0), chunk("hsl", k, k == 0), "ah%d" % k)
+    ts(R("bc", 0, 16, 2), R("cj", 0, 8), 0.0, A.mult, R("tm", 0, 1), A.add)
+    ts(R("bc", 1, 16, 2), R("cj", 0, 8), 0.0, A.mult, R("tm", 1, 2), A.add)
+    ts(R("z16h"), R("z1"), 16.0, A.mult)
+    ts(R("zm"), R("z1"), 65536.0, A.mult)
+    ts(R("zy"), R("z1"), -32768.0, A.mult)
+    ts(R("ixf"), R("ia"), 0.0, A.is_equal, -32768.0, A.mult)
+    cp(R("n0", 0, 1), R("cni", 0, 1))
+    fill(R("W", HB + 3072, HB + 4096), 0.0)
+    ts(col(0), R("tgb", 0, 1), -1.0, A.mult)
+
+    def late_constants():
+        cp(col(1), R("tei", 0, 1))
+        fill(R("ck", 0, 192, 2), 512.0)
+        for t in range(NS):
+            ts(R("ck", 64 * t + 1, 64 * t + 64, 2), R("cj"), float(XO[t] - HB), A.add)
+        for t in range(1, NS):
+            ts(R("cts", 256 * t, 256 * t + 256), R("cts", 0, 256), 31.0 * t, A.add)
+
+    def sums(ps, buf, lo):
+        mm(R(ps, 0, 64), R("ident"), R("ce"), True, False)
+        compact(R(ps, 0, 64), "z1", buf, lo, lo + 1024, False, True)
+
+    def ring(out):
+        ts(out, odd("eo"), 1983.5, A.min, 1.0 / 128, A.mult)
+
+    def hash_a(t):
+        tt(R("w0"), ("ind", R("so"), R("bc")), R("cts", 256 * t, 256 * t + 256), A.add)
+
+    def hash_b():
+        ts(R("w"), R("w0"), 4095, A.bitwise_and)
+        ts(R("pw2", 0, 256), R("w"), 128.0, A.add)
+        tt(R("pw"), R("w"), R("pw2", 0, 256), A.mult)
+        ts(R("h"), R("pw"), 7, A.logical_shift_right, 4095, A.bitwise_and)
+
+    def fallback_wide(t):
+        x = XO[t]
+        mm(R("pzw"), R("ident"), R("W", x, x + C), True, False)
+        mm(R("pzw"), R("nident"), R("mv", C * t, C * t + C), False, True)
+        act(R("W", x + C, x + 2 * C), R("pzw"), F.Abs)
+        act(R("W", x + 2 * C, x + 3 * C), R("W", x + C, x + 2 * C), F.Abs, bias=col(0))
+
+    def ring_counts(ncol):
+        ts(R("zn"), R("z1"), ncol, A.mult, 1.0 / 4096, A.mult)
+        compact(R("pp", 0, 32), "zn", "eq", 0, C, True, True)
+
+    def ring_columns():
+        mm(R("po", 0, 256), R("zero"), R("tie"), True, False)
+        for i in range(NT):
+            mm(R("po", 32 * i, 32 * i + 32), R("ident"), R("kb"), False, False)
+
+    def try_places():
+        for i in range(NT):
+            tt(R("prod", 32 * i, 32 * i + 32), R("h", 32 * i, 32 * i + 32), R("pp", 0, 32), A.mult)
+        ts(R("plh"), R("prod"), 1280.0 - 2047.5 / 4096, A.add)
+        mm(R("po", 0, 256), R("i16h"), R("plh"), False, True)
+
+    def open_keys(t):
+        mm(R("pw2"), R("ident"), R("W", XO[t], XO[t] + C), True, True)
+        for pk, i in (("pka", 0), ("pes", 4)):
+            mm(R(pk, 0, 64), R("ident"), R("tie", 32 * i, 32 * i + 64), True, False)
+            mm(R(pk, 0, 32), R("ixf"), odd("so"), False, False)
+            mm(R(pk, 32, 64), R("ixf"), odd("so"), False, False)
+
+    def relay(q, eng):
+        out, a = R("W", HB + q, HB + 3072, 16), R("hsl", 8 + M * q, 8 + M * q + M)
+        if eng == "v":
+            cp(out, a)
+        else:
+            act(out, a, F.Copy)
+
+    act(R("yb", C, 2 * C), R("yb", 0, C), F.Abs, bias=col(0))
+    sums("pes", "yb", 0)
+    cp(odd("eo"), R("pes", 32, 64))
+    cp(odd("so"), R("pes", 0, 32))
+    ring(R("k16"))
+    ring(R("ki"))
+    act(R("eq"), ("ind", R("id16"), R("k16")), F.Identity)
+    hash_a(0)
+    cp(R("kb"), R("ki"))
+    fallback_wide(0)
+    ring_columns()
+    hash_b()
+    sums("pze", "W", XO[0] + C)
+    for q in range(*CH[0]):
+        relay(q, "s")
+    late_constants()
+    ring_counts(R("hsl", 7, 8))
+    try_places()
+    open_keys(0)
+    ts(R("off"), R("po", 0, 256), -20480.0, A.add)
+    for k in range(1, len(CH)):
+        for j, q in enumerate(range(*CH[k])):
+            relay(q, "s" if j % 3 == 1 else "v")
+
+    for t in range(NS):
+        x0 = XO[t]
+
+        def sub(i, a=0, b=32):
+            tt(R("d", C * i + 16 * a, C * i + 16 * b), ("ind", HIST, R("off", 32 * i + a, 32 * i + b)),
+               R("W", x0 + 16 * a, x0 + 16 * b), A.subtract)
+
+        def mag(i, a=0, b=32):
+            act(R("ad", C * i + 16 * a, C * i + 16 * b), R("d", C * i + 16 * a, C * i + 16 * b), F.Abs)
+
+        def take(i):
+            act(R("d", C * i, C * i + C), ("ind", HIST, R("off", 32 * i, 32 * i + 32)), F.Copy)
+
+        def top(i):
+            tt(R("ad", C * i, C * i + C), R("d", C * i, C * i + C), R("pw2"), A.max)
+
+        def low(pk, i, tie=True):
+            if tie:
+                mm(R(pk, 0, 64), R("ident"), R("tie", 32 * i, 32 * i + 64), True, False)
+            mm(R(pk, 0, 64), R("i16h"), R("plh", 32 * i, 32 * i + 64), False, False)
+
+        def keys(pk, z, buf, i, stop):
+            compact(R(pk, 0, 64), z, buf, C * i, C * i + 2 * C, False, stop)
+
+        low("pka", 0, tie=False)
+        low("pes", 4, tie=False)
+        low("pkb", 2)
+        take(0)
+        take(1)
+        sub(2)
+        sub(3)
+        keys("pka", "zy", "d", 0, False)
+        mag(2)
+        take(4)
+        mag(3)
+        top(0)
+        top(1)
+        keys("pka", "zm", "ad", 0, True)
+        keys("pkb", "zd", "ad", 2, True)
+        sub(6)
+        take(5)
+        mag(6)
+        top(4)
+        cp(R("run"), R("pka", 0, 64))
+        keys("pes", "zy", "d", 4, False)
+        sub(7, 0, 16)
+        tt(R("run2"), R("run"), R("pkb", 0, 64), A.max)
+        top(5)
+        keys("pes", "zm", "ad", 4, True)
+        low("pkb", 6)
+        sub(7, 16, 32)
+        mag(7, 0, 16)
+        mag(7, 16, 32)
+        keys("pkb", "zd", "ad", 6, True)
+        cp(R("si"), odd("so"))
+        tt(even("so"), R("pze", 0, 32), odd("so"), A.subtract)
+        ts(R("sm"), R("si"), 63, A.bitwise_and)
+        tt(R("tm"), R("pze", 32, 64), odd("eo"), A.subtract)
+        ts(R("bnd"), R("sm"), col(1), A.mult)
+        cp(even("eo"), R("tm"))
+        tt(odd("mk"), R("tm"), R("bnd"), A.is_le)
+        tt(R("tm"), R("bnd"), odd("eo"), A.add)
+        scan(R("cf"), R("mk"), R("ck", 64 * t, 64 * t + 64), 0.0, A.mult, A.add)
+        scan(R("ef"), R("mk"), R("eo"), 0.0, A.mult, A.add)
+        scan(R("sf"), R("mk"), R("so"), 0.0, A.mult, A.add)
+        tt(R("run"), R("run2"), R("pes", 0, 64), A.max)
+        tt(R("run2"), R("run"), R("pkb", 0, 64), A.max)
+        tt(R("best"), R("run2", 0, 32), R("run2", 32, 64), A.max)
+        ts(R("wp"), R("best"), 0xFF0, A.bitwise_and)
+        tt(R("wc"), R("wp"), R("kb"), A.add)
+        cp(R("w16"), R("wc"))
+        act(R("yb", C, 2 * C), ("ind", HIST, R("w16")), F.Abs, bias=col(0))
+        cp(R("yb", 0, C), ("ind", HIST, R("w16")))
+        tt(even("cf"), R("wc"), odd("cf"), A.subtract)
+        sums("pes", "yb", 0)
+        tt(odd("mk"), R("pes", 32, 64), R("tm"), A.is_le)
+        tt(even("ef"), R("pes", 32, 64), odd("ef"), A.subtract)
+        scan(R("co"), R("mk"), R("cf"), 0.0, A.mult, A.add)
+        scan(R("eo"), R("mk"), R("ef"), 0.0, A.mult, A.add)
+        ts(R("c16"), odd("co"), float(HB - XO[t]), A.add)
+        ring(R("k16"))
+        last = t == NS - 1
+        xn = R("xout") if last else R("W", XO[t + 1], XO[t + 1] + C)
+        act(R("eq"), ("ind", R("id16"), R("k16")), F.Identity, accum=R("cnt", 0, 1))
+        cp(xn, ("ind", R("W", XO[t], HB + 4096), R("c16")))
+        nn = R("n%d" % (t + 1), 0, 1)
+        if last:
+            store("y", "sx", T.yx[:], xn)
+            ts(nn, R("cnt", 0, 1), R("n%d" % t, 0, 1), A.add, 256.0, A.min)
+            store("s", "sn", T.yn[:], nn)
+            break
+        s = str(t + 1)
+        ring(R("ki"))
+        mm(R("pzw"), R("ident"), R("eq"), True, True)
+        ts(nn, R("cnt", 0, 1), R("n%d" % t, 0, 1), A.add, 256.0, A.min)
+        scan(R("u"), R("eq"), R("eq"), R("n%d" % t, 0, 1), A.add, A.max)
+        send(nn, R("nl" + s, 0, 1), "an" + s)
+        send(xn, R("xl" + s), "ax" + s)
+        cp(R("kb"), R("ki"))
+        tt(R("m"), R("u"), R("pzw"), A.mult)
+        mm(R("pp", 0, 32), R("ident"), R("kb"), True, False)
+        compact(R("pp", 0, 32), "z16h", "m", 0, C, False, True)
+        tt(even("sf"), R("pes", 0, 32), odd("sf"), A.subtract)
+        scan(R("so"), R("mk"), R("sf"), 0.0, A.mult, A.add)
+        hash_a(t + 1)
+        ts(R("os" + s), R("pp", 0, 32), -16.0, A.add)
+        send(R("os" + s), R("ol" + s), "ao" + s)
+        fallback_wide(t + 1)
+        ring_columns()
+        hash_b()
+        ring_counts(R("nl" + s, 0, 1))
+        sums("pze", "W", XO[t + 1] + C)
+        try_places()
+        open_keys(t + 1)
+        cp(("ind", R("W", HB, HB + 12288), R("ol" + s)), R("xl" + s))
+        ts(R("off"), R("po", 0, 256), -20480.0, A.add)
+
+    for sem in ("qv", "qs", "qp", "qg", "sent"):
+        g.wait_ge(T.sem[sem], count[sem])
+    for sem in LOADS:
+        g.wait_ge(T.sem[sem], 16)
+    for sem in ARRIVE:
+        g.wait_ge(T.sem[sem], n_in)

@@ -1,28 +1,31 @@
 from concourse.mybir import AluOpType as A, ActivationFunctionType as F
 
 C, NT, NS, M = 512, 8, 3, 192
-HB = 3 * 1536
-XO = [2 * 1536, 1536, 0]
-CH = [(0, 4), (4, 11), (11, 16)]
+RB = 2 * 1536
+XO = [RB + 12288 + 16, 1536, 0]
+HB = [XO[0] + 1024, RB, RB]
+HN = [16 * M, 4096, 4096]
+CH = [(0, 6), (6, 12), (12, 16)]
 BF, F32, I32, U16, F16 = "bfloat16", "float32", "int32", "uint16", "float16"
 
 SBUF = {
-    BF: {"W": HB + 12288, "hsb": 8 + 3072, "hsl": 8 + 3072, "mv": 1536, "xout": 512, "d": 4096, "ad": 4096, "yb": 1024,
-         "eq": 512, "tgb": 16, "ident": 128, "nident": 128, "zero": 128, "id16": 16,
-         "z1": 144, "zd": 144, "zm": 144, "zy": 144, "zn": 144, "ce": 64, "tie": 256, "kb": 32,
+    BF: {"W": HB[0] + HN[0], "hsb": 3072, "xs": 16 + 2048, "mv": 1536, "xn0": 512, "xout": 512, "d": 4096,
+         "ad": 4096, "yb": 1024, "eq": 512, "ident": 128, "nident": 128, "zero": 128, "id16": 16,
+         "z1": 144, "zd": 144, "zm": 144, "zy": 144, "zq": 144, "zn": 144, "ce": 64, "tie": 256, "kb": 32,
          "xl1": 512, "xl2": 512},
-    F32: {"col": 16, "ixf": 128, "cts": 768, "cj": 32, "ck": 192, "mk": 64, "eo": 64, "so": 64, "co": 64,
+    F32: {"col": 16, "ixf": 128, "cts": 768, "cj": 32, "ck": 192, "mk": 64, "sto": 128, "st0": 128, "st1": 128,
+          "fz": 64, "fzl": 64, "co": 64,
           "ef": 64, "sf": 64, "cf": 64, "tm": 32, "bnd": 32, "prod": 256, "run": 64, "run2": 64, "wc": 32, "cnt": 8,
-          "n0": 8, "n1": 8, "n2": 8, "n3": 8, "nl1": 8, "nl2": 8},
-    I32: {"tei": 8, "cni": 8, "ia": 128, "ib": 32, "ct": 256, "ki": 32, "si": 32, "sm": 32, "w0": 256, "w": 256, "pw": 256,
-          "h": 256, "best": 32, "wp": 32},
+          "na0": 8, "na1": 8, "n1": 8, "n2": 8, "n3": 8, "nl0": 8, "nl1": 8, "nl2": 8},
+    I32: {"tc": 8, "tcl": 8, "ia": 128, "ib": 32, "ct": 256, "ki": 32, "si": 32, "sm": 32, "w0": 256, "w": 256, "pw": 256,
+          "h": 256, "ho": 256, "hl": 256, "best": 32, "wp": 32},
     U16: {"bc": 16, "k16": 32, "c16": 32, "w16": 32, "off": 256, "os1": 32, "os2": 32, "ol1": 32, "ol2": 32},
     F16: {"plh": 256, "i16h": 128, "z16h": 144, "u": 512, "m": 512},
 }
 SCRATCH = {name: ("sbuf", [128, n], dt) for dt, bufs in SBUF.items() for name, n in bufs.items()}
 SCRATCH.update({name: ("psum", [128, 512], F32) for name in ("pka", "pkb", "pes", "pzw", "pze", "po", "pp", "pw2")})
-LOADS = ["lh%d" % k for k in range(len(CH))] + ["lcn", "lx", "ly", "ltg", "lte", "lmv", "sx", "sn"]
-ARRIVE = ["ah%d" % k for k in range(len(CH))] + ["an1", "an2", "ax1", "ax2", "ao1", "ao2"]
+LOADS = ["lh%d" % k for k in range(len(CH))] + ["lcn", "lx", "ltg", "lte", "lm0", "lmv", "sx", "sn"]
+ARRIVE = ["ax0", "atc", "as0", "ah0", "az0", "af0", "ah", "ast", "axh", "anh", "an1", "an2", "ax1", "ax2", "ao1", "ao2"]
 SEMAPHORES = ["qv", "qs", "qp", "qg", "sent"] + LOADS + ARRIVE
 
 
@@ -35,21 +38,17 @@ def rank_program(g, core, T, topo):
     if rank is None:
         return
     n_ranks = len(T.cores)
-    dst = T.cores[(rank - 1) % n_ranks]
-    src = T.cores[(rank + 1) % n_ranks]
-    rid, pid = topo.addr(dst, core)
-    mask = topo.mask(core, dst)
-    n_out, n_in = len(topo.engines(core, dst)), len(topo.engines(src, core))
     Q = {"v": g.vector, "s": g.scalar, "p": g.tensor, "g": g, "y": g.sync}
     count = {"qv": 0, "qs": 0, "qp": 0, "qg": 0, "sent": 0}
     known = {q: {} for q in Q}
     log = {name: [] for name in SCRATCH}
+    arrivals = {}
 
     def ap(r):
         return T[r[0]][:, r[1]:r[2]:r[3]] if r[3] != 1 else T[r[0]][:, r[1]:r[2]]
 
     def cols(r):
-        return set(range(512)) if SCRATCH[r[0]][0] == "psum" else set(range(r[1], r[2], r[3]))
+        return set(range(r[1], r[2], r[3]))
 
     def order(q, reads, writes):
         need = {}
@@ -59,7 +58,8 @@ def rank_program(g, core, T, topo):
                 for (c2, w2, q2, sem, val, clock) in log[r[0]]:
                     if q == "p" and q2 == "p":
                         continue
-                    if (wr or w2 or (psum and q2 != q)) and known[q].get(sem, 0) < val and not cs.isdisjoint(c2):
+                    clash = (psum and q2 != q) or ((wr or w2) and not cs.isdisjoint(c2))
+                    if clash and known[q].get(sem, 0) < val:
                         if val > need.get(sem, (0, None))[0]:
                             need[sem] = (val, clock)
         for sem, (val, clock) in sorted(need.items(), key=lambda e: -sum(e[1][1].values())):
@@ -111,15 +111,16 @@ def rank_program(g, core, T, topo):
         x, rx, _ = opnd(init)
         call("v", lambda: g.vector.tensor_tensor_scan(ap(out), ap(d0), ap(d1), x, op0, op1), [d0, d1] + rx, [out])
 
-    def act(out, a, func, bias=None, accum=None):
+    def act(out, a, func, bias=None, scale=None, accum=None):
         x, rx, ox = opnd(a)
-        kw = {}
-        if bias is not None:
-            kw["bias"] = ap(bias)
+        kw, more = {}, []
+        for key, val in (("bias", bias), ("scale", scale)):
+            if val is not None:
+                kw[key], r, _ = opnd(val)
+                more += r
         if accum is not None:
             kw["accum_out"] = ap(accum)
-        call("s", lambda: g.scalar.activation(ap(out), x, func, **kw),
-             rx + ox + ([bias] if bias else []), [out] + ([accum] if accum else []))
+        call("s", lambda: g.scalar.activation(ap(out), x, func, **kw), rx + ox + more, [out] + ([accum] if accum else []))
 
     def mm(out, lhs, rhs, start, stop):
         call("p", lambda: g.tensor.matmul(ap(out), ap(lhs), ap(rhs), start, stop), [lhs, rhs], [out])
@@ -137,46 +138,54 @@ def rank_program(g, core, T, topo):
         order(q, [a], [])
         Q[q].dma_start(dram, ap(a)).then_inc(T.sem[sem], 16)
 
-    def send(a, land, sem):
+    def send(step, a, land, sem):
+        dst, src = T.cores[(rank + step) % n_ranks], T.cores[(rank - step) % n_ranks]
+        rid, pid = topo.addr(dst, core)
         order("g", [a], [])
-        g.remote_dma(ap(land), ap(a), T.sem[sem], T.sem.sent, pid, rid, mask)
-        count["sent"] += n_out
-        log[land[0]].append((cols(land), True, "dma", sem, n_in, {}))
+        g.remote_dma(ap(land), ap(a), T.sem[sem], T.sem.sent, pid, rid, topo.mask(core, dst))
+        count["sent"] += len(topo.engines(core, dst))
+        arrivals[sem] = len(topo.engines(src, core))
+        log[land[0]].append((cols(land), True, "dma", sem, arrivals[sem], {}))
 
     def col(j):
         return R("col", j, j + 1)
 
-    def odd(name):
-        return R(name, 1, 64, 2)
+    def odd(name, lo=0):
+        return R(name, lo + 1, lo + 64, 2)
 
-    def even(name):
-        return R(name, 0, 64, 2)
+    def even(name, lo=0):
+        return R(name, lo, lo + 64, 2)
 
-    def chunk(name, k, head=False):
-        return R(name, 0 if head else 8 + M * CH[k][0], 8 + M * CH[k][1])
+    HIST = [R("W", HB[t], HB[t] + HN[t]) for t in range(NS)]
+    TG = [R("W", XO[0] - 1, XO[0]), R("xs", 15, 16), R("xs", 15, 16)]
+    ST = ["st0", "st1", "st1"]
+    TE = [col(0), col(1), col(1)]
+    N_OLD = [R("na0", 0, 1), R("n1", 0, 1), R("n2", 0, 1)]
+    N_NEW = [R("na1", 0, 1), R("n2", 0, 1), R("n3", 0, 1)]
+    FZ = ["fzl", "pze", "pze"]
 
-    HIST = R("W", HB, HB + 4096)
-
-    for k in range(len(CH)):
-        load("y", "lh%d" % k, chunk("hsb", k), T.hs[:, M * CH[k][0]:M * CH[k][1]])
-    load("s", "lcn", R("cni", 0, 1), T.cn[:])
-    load("s", "ly", R("yb", 0, C), T.x0[:])
-    load("s", "ltg", R("tgb", 0, 1), T.tg[:])
-    load("s", "lx", R("W", XO[0], XO[0] + C), T.x0[:])
-    load("y", "lte", R("tei", 0, 1), T.te[:])
-    load("y", "lmv", R("mv"), T.dv[:])
+    load("s", "lte", R("tc", 0, 1), T.te[:])
+    load("s", "lcn", R("tc", 1, 2), T.cn[:])
+    load("y", "ltg", R("xs", 15, 16), T.tg[:])
+    load("y", "lx", R("xs", 16, 16 + C), T.x0[:])
+    load("y", "lm0", R("mv", 0, C), T.dv[:, 0:C])
+    for k, (a, b) in enumerate(CH):
+        load("y", "lh%d" % k, R("hsb", M * a, M * b), T.hs[:, M * a:M * b])
 
     call("g", lambda: g.iota(ap(R("ia")), [[-1, 128]], 0, 1), [], [R("ia")])
     call("g", lambda: g.iota(ap(R("ct")), [[97, NT], [80, 32]], 0, 0), [], [R("ct")])
     call("g", lambda: g.iota(ap(R("tie")), [[-4096, NT], [0, 32]], 4096 * (NT - 1) - 20480, 0,
                              allow_small_or_imprecise_dtypes=True), [], [R("tie")])
-    fill(R("hsb", 0, 8), 0.0)
+    send(1, R("tc", 0, 2), R("tcl", 0, 2), "atc")
+    send(1, R("xs", 15, 16 + C), R("W", XO[0] - 1, XO[0] + C), "ax0")
     fill(R("z1"), 0.0)
     fill(R("ce", 0, 32), 0.0)
     fill(R("ce", 32, 64), -63.5)
     fill(R("mk"), 0.0)
-    fill(R("so"), 0.0)
+    fill(R("sto"), 0.0)
     fill(R("zero"), 0.0)
+    fill(R("W", RB + 16 * M, RB + 4096), 0.0)
+    fill(R("ck", 0, 192, 2), 512.0)
     ts(R("ib", 0, 8), R("ia", 0, 128, 16), 4, A.arith_shift_right)
     ts(R("ib", 8, 24), R("ia", 0, 16), 15, A.bitwise_and)
     ts(R("ident"), R("ia"), 0.0, A.is_equal)
@@ -191,52 +200,57 @@ def rank_program(g, core, T, topo):
     ts(R("zd"), R("z1"), 32768.0, A.mult)
     ts(R("tm", 0, 2), R("cj", 0, 2), 2.0, A.mult, 1.0, A.add)
     ts(R("cts", 0, 256), R("ct"), col(3), A.add)
-    cp(R("hsb", 7, 8), R("cni", 0, 1))
-    for k in range(len(CH)):
-        send(chunk("hsb", k, k == 0), chunk("hsl", k, k == 0), "ah%d" % k)
     ts(R("bc", 0, 16, 2), R("cj", 0, 8), 0.0, A.mult, R("tm", 0, 1), A.add)
     ts(R("bc", 1, 16, 2), R("cj", 0, 8), 0.0, A.mult, R("tm", 1, 2), A.add)
     ts(R("z16h"), R("z1"), 16.0, A.mult)
     ts(R("zm"), R("z1"), 65536.0, A.mult)
     ts(R("zy"), R("z1"), -32768.0, A.mult)
+    ts(R("zq"), R("z1"), 1.0 / 4096, A.mult)
     ts(R("ixf"), R("ia"), 0.0, A.is_equal, -32768.0, A.mult)
-    cp(R("n0", 0, 1), R("cni", 0, 1))
-    fill(R("W", HB + 3072, HB + 4096), 0.0)
-    ts(col(0), R("tgb", 0, 1), -1.0, A.mult)
-
-    def late_constants():
-        cp(col(1), R("tei", 0, 1))
-        fill(R("ck", 0, 192, 2), 512.0)
-        for t in range(NS):
-            ts(R("ck", 64 * t + 1, 64 * t + 64, 2), R("cj"), float(XO[t] - HB), A.add)
-        for t in range(1, NS):
-            ts(R("cts", 256 * t, 256 * t + 256), R("cts", 0, 256), 31.0 * t, A.add)
+    for t in range(NS):
+        ts(R("ck", 64 * t + 1, 64 * t + 64, 2), R("cj"), float(XO[t] - HB[t]), A.add)
+    for t in range(1, NS):
+        ts(R("cts", 256 * t, 256 * t + 256), R("cts", 0, 256), 31.0 * t, A.add)
+    cp(col(1), R("tc", 0, 1))
+    cp(R("nl0", 0, 1), R("tc", 1, 2))
 
     def sums(ps, buf, lo):
         mm(R(ps, 0, 64), R("ident"), R("ce"), True, False)
         compact(R(ps, 0, 64), "z1", buf, lo, lo + 1024, False, True)
 
-    def ring(out):
-        ts(out, odd("eo"), 1983.5, A.min, 1.0 / 128, A.mult)
+    def ring(out, t):
+        ts(out, odd(ST[t]), 1983.5, A.min, 1.0 / 128, A.mult)
 
-    def hash_a(t):
-        tt(R("w0"), ("ind", R("so"), R("bc")), R("cts", 256 * t, 256 * t + 256), A.add)
+    def one_hot(eng="s", a=0, b=32, accum=None):
+        out, src = R("eq", 16 * a, 16 * b), ("ind", R("id16"), R("k16", a, b))
+        if eng == "s":
+            act(out, src, F.Identity, accum=accum)
+        else:
+            cp(out, src)
 
-    def hash_b():
-        ts(R("w"), R("w0"), 4095, A.bitwise_and)
-        ts(R("pw2", 0, 256), R("w"), 128.0, A.add)
-        tt(R("pw"), R("w"), R("pw2", 0, 256), A.mult)
-        ts(R("h"), R("pw"), 7, A.logical_shift_right, 4095, A.bitwise_and)
+    def make_hash(st, t, h):
+        halves = [(0, 128), (128, 256)]
+        for a, b in halves:
+            tt(R("w0", a, b), ("ind", R(st, 64, 128), R("bc", 0, 8)), R("cts", 256 * t + a, 256 * t + b), A.add)
+        for a, b in halves:
+            ts(R("w", a, b), R("w0", a, b), 4095, A.bitwise_and)
+        for a, b in halves:
+            ts(R("pze", a, b), R("w", a, b), 128.0, A.add)
+        for a, b in halves:
+            tt(R("pw", a, b), R("w", a, b), R("pze", a, b), A.mult)
+        for a, b in halves:
+            ts(R(h, a, b), R("pw", a, b), 7, A.logical_shift_right, 4095, A.bitwise_and)
 
-    def fallback_wide(t):
-        x = XO[t]
-        mm(R("pzw"), R("ident"), R("W", x, x + C), True, False)
-        mm(R("pzw"), R("nident"), R("mv", C * t, C * t + C), False, True)
-        act(R("W", x + C, x + 2 * C), R("pzw"), F.Abs)
-        act(R("W", x + 2 * C, x + 3 * C), R("W", x + C, x + 2 * C), F.Abs, bias=col(0))
+    def fallback_wide(x, mv, buf, lo):
+        mm(R("pzw"), R("ident"), x, True, False)
+        mm(R("pzw"), R("nident"), mv, False, True)
+        act(R(buf, lo, lo + C), R("pzw"), F.Abs)
+        act(R(buf, lo + C, lo + 2 * C), R(buf, lo, lo + C), F.Abs, bias=TG[1], scale=-1.0)
 
-    def ring_counts(ncol):
-        ts(R("zn"), R("z1"), ncol, A.mult, 1.0 / 4096, A.mult)
+    def ring_weights(t):
+        act(R("zn"), R("zq"), F.Identity, scale=R("nl%d" % t, 0, 1))
+
+    def ring_counts():
         compact(R("pp", 0, 32), "zn", "eq", 0, C, True, True)
 
     def ring_columns():
@@ -244,62 +258,73 @@ def rank_program(g, core, T, topo):
         for i in range(NT):
             mm(R("po", 32 * i, 32 * i + 32), R("ident"), R("kb"), False, False)
 
-    def try_places():
+    def try_places(h, between=None):
         for i in range(NT):
-            tt(R("prod", 32 * i, 32 * i + 32), R("h", 32 * i, 32 * i + 32), R("pp", 0, 32), A.mult)
-        ts(R("plh"), R("prod"), 1280.0 - 2047.5 / 4096, A.add)
+            tt(R("prod", 32 * i, 32 * i + 32), R(h, 32 * i, 32 * i + 32), R("pp", 0, 32), A.mult)
+        for a in (0, 128):
+            ts(R("plh", a, a + 128), R("prod", a, a + 128), 1280.0 - 2047.5 / 4096, A.add)
         mm(R("po", 0, 256), R("i16h"), R("plh"), False, True)
+        if between:
+            between()
+        ts(R("off"), R("po", 0, 256), -20480.0, A.add)
 
     def open_keys(t):
         mm(R("pw2"), R("ident"), R("W", XO[t], XO[t] + C), True, True)
         for pk, i in (("pka", 0), ("pes", 4)):
             mm(R(pk, 0, 64), R("ident"), R("tie", 32 * i, 32 * i + 64), True, False)
-            mm(R(pk, 0, 32), R("ixf"), odd("so"), False, False)
-            mm(R(pk, 32, 64), R("ixf"), odd("so"), False, False)
+            mm(R(pk, 0, 32), R("ixf"), odd(ST[t], 64), False, False)
+            mm(R(pk, 32, 64), R("ixf"), odd(ST[t], 64), False, False)
 
     def relay(q, eng):
-        out, a = R("W", HB + q, HB + 3072, 16), R("hsl", 8 + M * q, 8 + M * q + M)
+        out, a = R("W", HB[0] + q, HB[0] + 16 * M, 16), R("hsb", M * q, M * q + M)
         if eng == "v":
             cp(out, a)
         else:
             act(out, a, F.Copy)
 
-    act(R("yb", C, 2 * C), R("yb", 0, C), F.Abs, bias=col(0))
-    sums("pes", "yb", 0)
-    cp(odd("eo"), R("pes", 32, 64))
-    cp(odd("so"), R("pes", 0, 32))
-    ring(R("k16"))
-    ring(R("ki"))
-    act(R("eq"), ("ind", R("id16"), R("k16")), F.Identity)
-    hash_a(0)
-    cp(R("kb"), R("ki"))
-    fallback_wide(0)
-    ring_columns()
-    hash_b()
-    sums("pze", "W", XO[0] + C)
+    act(R("xs", 16 + C, 16 + 2 * C), R("xs", 16, 16 + C), F.Abs, bias=TG[1], scale=-1.0)
+    sums("pes", "xs", 16)
+    ring_weights(0)
+    cp(odd("sto"), R("pes", 32, 64))
+    cp(odd("sto", 64), R("pes", 0, 32))
+    send(1, R("sto"), R("st0"), "as0")
     for q in range(*CH[0]):
         relay(q, "s")
-    late_constants()
-    ring_counts(R("hsl", 7, 8))
-    try_places()
+    make_hash("sto", 0, "ho")
+    send(1, R("ho"), R("hl"), "ah0")
+    fallback_wide(R("xs", 16, 16 + C), R("mv", 0, C), "xs", 16 + 2 * C)
+    send(1, R("xs", 16 + 2 * C, 16 + 3 * C), R("W", XO[0] + C, XO[0] + 2 * C), "az0")
+    sums("pze", "xs", 16 + 2 * C)
+    for q in range(CH[0][1], 16):
+        relay(q, "s" if q % 4 == 1 else "v")
+    act(R("fz"), R("pze", 0, 64), F.Copy)
+    send(1, R("fz"), R("fzl"), "af0")
+    send(-1, HIST[0], R("W", RB, RB + 16 * M), "ah")
+    order("y", [R("st0")], [])
+    load("y", "lmv", R("mv", C, 3 * C), T.dv[:, C:3 * C])
+    ring(R("k16"), 0)
+    one_hot()
+    ring(R("ki"), 0)
+    cp(R("kb"), R("ki"))
+    cp(col(0), R("tcl", 0, 1))
+    cp(N_OLD[0], R("tcl", 1, 2))
+    ring_columns()
+    ring_counts()
+    try_places("hl")
     open_keys(0)
-    ts(R("off"), R("po", 0, 256), -20480.0, A.add)
-    for k in range(1, len(CH)):
-        for j, q in enumerate(range(*CH[k])):
-            relay(q, "s" if j % 3 == 1 else "v")
 
     for t in range(NS):
-        x0 = XO[t]
+        x0, st = XO[t], ST[t]
 
         def sub(i, a=0, b=32):
-            tt(R("d", C * i + 16 * a, C * i + 16 * b), ("ind", HIST, R("off", 32 * i + a, 32 * i + b)),
+            tt(R("d", C * i + 16 * a, C * i + 16 * b), ("ind", HIST[t], R("off", 32 * i + a, 32 * i + b)),
                R("W", x0 + 16 * a, x0 + 16 * b), A.subtract)
 
         def mag(i, a=0, b=32):
             act(R("ad", C * i + 16 * a, C * i + 16 * b), R("d", C * i + 16 * a, C * i + 16 * b), F.Abs)
 
         def take(i):
-            act(R("d", C * i, C * i + C), ("ind", HIST, R("off", 32 * i, 32 * i + 32)), F.Copy)
+            act(R("d", C * i, C * i + C), ("ind", HIST[t], R("off", 32 * i, 32 * i + 32)), F.Copy)
 
         def top(i):
             tt(R("ad", C * i, C * i + C), R("d", C * i, C * i + C), R("pw2"), A.max)
@@ -311,6 +336,10 @@ def rank_program(g, core, T, topo):
 
         def keys(pk, z, buf, i, stop):
             compact(R(pk, 0, 64), z, buf, C * i, C * i + 2 * C, False, stop)
+
+        def new_sums():
+            tt(even("sf"), R("pes", 0, 32), odd("sf"), A.subtract)
+            scan(R(st, 64, 128), R("mk"), R("sf"), 0.0, A.mult, A.add)
 
         low("pka", 0, tie=False)
         low("pes", 4, tie=False)
@@ -342,72 +371,94 @@ def rank_program(g, core, T, topo):
         mag(7, 0, 16)
         mag(7, 16, 32)
         keys("pkb", "zd", "ad", 6, True)
-        cp(R("si"), odd("so"))
-        tt(even("so"), R("pze", 0, 32), odd("so"), A.subtract)
+        cp(R("si"), odd(st, 64))
+        tt(even(st, 64), R(FZ[t], 0, 32), odd(st, 64), A.subtract)
         ts(R("sm"), R("si"), 63, A.bitwise_and)
-        tt(R("tm"), R("pze", 32, 64), odd("eo"), A.subtract)
-        ts(R("bnd"), R("sm"), col(1), A.mult)
-        cp(even("eo"), R("tm"))
+        tt(R("tm"), R(FZ[t], 32, 64), odd(st), A.subtract)
+        ts(R("bnd"), R("sm"), TE[t], A.mult)
+        cp(even(st), R("tm"))
         tt(odd("mk"), R("tm"), R("bnd"), A.is_le)
-        tt(R("tm"), R("bnd"), odd("eo"), A.add)
+        tt(R("tm"), R("bnd"), odd(st), A.add)
         scan(R("cf"), R("mk"), R("ck", 64 * t, 64 * t + 64), 0.0, A.mult, A.add)
-        scan(R("ef"), R("mk"), R("eo"), 0.0, A.mult, A.add)
-        scan(R("sf"), R("mk"), R("so"), 0.0, A.mult, A.add)
+        scan(R("ef"), R("mk"), R(st, 0, 64), 0.0, A.mult, A.add)
+        scan(R("sf"), R("mk"), R(st, 64, 128), 0.0, A.mult, A.add)
         tt(R("run"), R("run2"), R("pes", 0, 64), A.max)
         tt(R("run2"), R("run"), R("pkb", 0, 64), A.max)
         tt(R("best"), R("run2", 0, 32), R("run2", 32, 64), A.max)
         ts(R("wp"), R("best"), 0xFF0, A.bitwise_and)
         tt(R("wc"), R("wp"), R("kb"), A.add)
         cp(R("w16"), R("wc"))
-        act(R("yb", C, 2 * C), ("ind", HIST, R("w16")), F.Abs, bias=col(0))
-        cp(R("yb", 0, C), ("ind", HIST, R("w16")))
+        act(R("yb", C, 2 * C), ("ind", HIST[t], R("w16")), F.Abs, bias=TG[t], scale=-1.0)
+        cp(R("yb", 0, C), ("ind", HIST[t], R("w16")))
         tt(even("cf"), R("wc"), odd("cf"), A.subtract)
         sums("pes", "yb", 0)
         tt(odd("mk"), R("pes", 32, 64), R("tm"), A.is_le)
         tt(even("ef"), R("pes", 32, 64), odd("ef"), A.subtract)
-        scan(R("co"), R("mk"), R("cf"), 0.0, A.mult, A.add)
-        scan(R("eo"), R("mk"), R("ef"), 0.0, A.mult, A.add)
-        ts(R("c16"), odd("co"), float(HB - XO[t]), A.add)
-        ring(R("k16"))
         last = t == NS - 1
-        xn = R("xout") if last else R("W", XO[t + 1], XO[t + 1] + C)
-        act(R("eq"), ("ind", R("id16"), R("k16")), F.Identity, accum=R("cnt", 0, 1))
-        cp(xn, ("ind", R("W", XO[t], HB + 4096), R("c16")))
-        nn = R("n%d" % (t + 1), 0, 1)
+        xn = [R("xn0"), R("W", XO[2], XO[2] + C), R("xout")][t]
+        picked = ("ind", R("W", XO[t], HB[t] + HN[t]), R("c16"))
         if last:
+            scan(R("co"), R("mk"), R("cf"), 0.0, A.mult, A.add)
+            scan(R(st, 0, 64), R("mk"), R("ef"), 0.0, A.mult, A.add)
+            ts(R("c16"), odd("co"), float(HB[t] - XO[t]), A.add)
+            ring(R("k16"), t)
+            one_hot(accum=R("cnt", 0, 1))
+            cp(xn, picked)
             store("y", "sx", T.yx[:], xn)
-            ts(nn, R("cnt", 0, 1), R("n%d" % t, 0, 1), A.add, 256.0, A.min)
-            store("s", "sn", T.yn[:], nn)
+            ts(N_NEW[t], R("cnt", 0, 1), N_OLD[t], A.add, 256.0, A.min)
+            store("s", "sn", T.yn[:], N_NEW[t])
             break
-        s = str(t + 1)
-        ring(R("ki"))
+        scan(R(st, 0, 64), R("mk"), R("ef"), 0.0, A.mult, A.add)
+        scan(R("co"), R("mk"), R("cf"), 0.0, A.mult, A.add)
+        ring(R("k16"), t)
+        one_hot("s", 0, 18)
+        ts(R("c16"), odd("co"), float(HB[t] - XO[t]), A.add)
+        one_hot("v", 18, 32)
+        act(xn, picked, F.Copy)
+        s, to = str(t + 1), -2 if t == 0 else -1
+        if t == 0:
+            new_sums()
+            send(-1, R("st0"), R("st1"), "ast")
+        else:
+            ring(R("ki"), t)
         mm(R("pzw"), R("ident"), R("eq"), True, True)
-        ts(nn, R("cnt", 0, 1), R("n%d" % t, 0, 1), A.add, 256.0, A.min)
-        scan(R("u"), R("eq"), R("eq"), R("n%d" % t, 0, 1), A.add, A.max)
-        send(nn, R("nl" + s, 0, 1), "an" + s)
-        send(xn, R("xl" + s), "ax" + s)
-        cp(R("kb"), R("ki"))
+        scan(R("u"), R("eq"), R("eq"), N_OLD[t], A.add, A.max)
+        if t == 0:
+            ring(R("ki"), t)
+        ts(N_NEW[t], R("u", C - 1, C), 256.0, A.min)
+        send(to, N_NEW[t], R("nl" + s, 0, 1), "an" + s)
         tt(R("m"), R("u"), R("pzw"), A.mult)
-        mm(R("pp", 0, 32), R("ident"), R("kb"), True, False)
-        compact(R("pp", 0, 32), "z16h", "m", 0, C, False, True)
-        tt(even("sf"), R("pes", 0, 32), odd("sf"), A.subtract)
-        scan(R("so"), R("mk"), R("sf"), 0.0, A.mult, A.add)
-        hash_a(t + 1)
+        cp(R("kb"), R("ki"))
+        send(to, xn, R("xl" + s), "ax" + s)
+        if t == 0:
+            send(-1, xn, R("W", XO[1], XO[1] + C), "axh")
+        compact(R("pp", 0, 32), "z16h", "m", 0, C, True, False)
+        mm(R("pp", 0, 32), R("ident"), R("kb"), False, True)
+        x1 = XO[t + 1]
+        if t == 1:
+            new_sums()
+            fallback_wide(xn, R("mv", 2 * C, 3 * C), "W", x1 + C)
         ts(R("os" + s), R("pp", 0, 32), -16.0, A.add)
-        send(R("os" + s), R("ol" + s), "ao" + s)
-        fallback_wide(t + 1)
+        send(to, R("os" + s), R("ol" + s), "ao" + s)
+        if t == 0:
+            send(-1, N_NEW[0], N_OLD[1], "anh")
+            ring(R("k16"), 1)
+            one_hot()
+            ring(R("ki"), 1)
+            cp(R("kb"), R("ki"))
+        make_hash(ST[t + 1], t + 1, "h")
         ring_columns()
-        hash_b()
-        ring_counts(R("nl" + s, 0, 1))
-        sums("pze", "W", XO[t + 1] + C)
-        try_places()
+        ring_weights(t + 1)
+        ring_counts()
+        if t == 0:
+            fallback_wide(R("W", x1, x1 + C), R("mv", C, 2 * C), "W", x1 + C)
+        try_places("h", lambda: cp(("ind", R("W", RB, RB + 12288), R("ol" + s)), R("xl" + s)))
         open_keys(t + 1)
-        cp(("ind", R("W", HB, HB + 12288), R("ol" + s)), R("xl" + s))
-        ts(R("off"), R("po", 0, 256), -20480.0, A.add)
+        sums("pze", "W", x1 + C)
 
     for sem in ("qv", "qs", "qp", "qg", "sent"):
         g.wait_ge(T.sem[sem], count[sem])
     for sem in LOADS:
         g.wait_ge(T.sem[sem], 16)
     for sem in ARRIVE:
-        g.wait_ge(T.sem[sem], n_in)
+        g.wait_ge(T.sem[sem], arrivals[sem])

@@ -6,12 +6,14 @@ XO = [RB + 12288 + 16, 1536, 0]
 HB = [XO[0] + 1024, RB, RB]
 HN = [16 * M, 4096, 4096]
 CH = [(0, 6), (6, 12), (12, 16)]
+JA = 16
+LEAD = 3
 BF, F32, I32, U16, F16 = "bfloat16", "float32", "int32", "uint16", "float16"
 
 SBUF = {
     BF: {"W": HB[0] + HN[0], "hsb": 3072, "xs": 16 + 2048, "mv": 1536, "xn0": 512, "xout": 512, "d": 4096,
-         "ad": 4096, "yb": 1024, "eq": 512, "ident": 128, "nident": 128, "zero": 128, "id16": 16,
-         "z1": 144, "zd": 144, "zm": 144, "zy": 144, "zq": 144, "zn": 144, "ce": 64, "tie": 256, "kb": 32,
+         "ad": 4096, "yb": 1024, "eq": 1024, "ident": 128, "nident": 128, "zero": 128, "id16": 16,
+         "z1": 144, "zd": 144, "zm": 144, "zy": 144, "zq": 144, "zn": 144, "ce": 64, "tie": 256, "tie2": 64, "kb": 32,
          "xl1": 512, "xl2": 512},
     F32: {"col": 16, "ixf": 128, "cts": 768, "cj": 32, "ck": 192, "mk": 64, "sto": 128, "st0": 128, "st1": 128,
           "fz": 64, "fzl": 64, "co": 64,
@@ -19,13 +21,15 @@ SBUF = {
           "na0": 8, "na1": 8, "n1": 8, "n2": 8, "n3": 8, "nl0": 8, "nl1": 8, "nl2": 8},
     I32: {"tc": 8, "tcl": 8, "ia": 128, "ib": 32, "ct": 256, "ki": 32, "si": 32, "sm": 32, "w0": 256, "w": 256, "pw": 256,
           "h": 256, "ho": 256, "hl": 256, "best": 32, "wp": 32},
-    U16: {"bc": 16, "k16": 32, "c16": 32, "w16": 32, "off": 256, "os1": 32, "os2": 32, "ol1": 32, "ol2": 32},
+    U16: {"bc": 16, "k16": 32, "c16": 32, "w16": 32, "off": 256,
+          "os1a": 32, "os1b": 32, "os2a": 32, "os2b": 32, "ol1a": 32, "ol1b": 32, "ol2a": 32, "ol2b": 32},
     F16: {"plh": 256, "i16h": 128, "z16h": 144, "u": 512, "m": 512},
 }
 SCRATCH = {name: ("sbuf", [128, n], dt) for dt, bufs in SBUF.items() for name, n in bufs.items()}
 SCRATCH.update({name: ("psum", [128, 512], F32) for name in ("pka", "pkb", "pes", "pzw", "pze", "po", "pp", "pw2")})
 LOADS = ["lh%d" % k for k in range(len(CH))] + ["lcn", "lx", "ltg", "lte", "lm0", "lmv", "sx", "sn"]
-ARRIVE = ["ax0", "atc", "as0", "ah0", "az0", "af0", "ah", "ast", "axh", "anh", "an1", "an2", "ax1", "ax2", "ao1", "ao2"]
+ARRIVE = ["ax0", "atc", "as0", "ah0", "az0", "af0", "ah", "ast", "axh", "anh", "an1", "an2",
+          "ax1a", "ax1b", "ax2a", "ax2b", "ao1a", "ao1b", "ao2a", "ao2b"]
 SEMAPHORES = ["qv", "qs", "qp", "qg", "sent"] + LOADS + ARRIVE
 
 
@@ -186,6 +190,8 @@ def rank_program(g, core, T, topo):
     fill(R("zero"), 0.0)
     fill(R("W", RB + 16 * M, RB + 4096), 0.0)
     fill(R("ck", 0, 192, 2), 512.0)
+    for a, b, v in ((0, JA, 4096), (JA, 2 * JA, 0), (2 * JA, 32 + JA, 4096), (32 + JA, 64, 0)):
+        fill(R("tie2", a, b), v - 20480.0)
     ts(R("ib", 0, 8), R("ia", 0, 128, 16), 4, A.arith_shift_right)
     ts(R("ib", 8, 24), R("ia", 0, 16), 15, A.bitwise_and)
     ts(R("ident"), R("ia"), 0.0, A.is_equal)
@@ -218,8 +224,8 @@ def rank_program(g, core, T, topo):
         mm(R(ps, 0, 64), R("ident"), R("ce"), True, False)
         compact(R(ps, 0, 64), "z1", buf, lo, lo + 1024, False, True)
 
-    def ring(out, t):
-        ts(out, odd(ST[t]), 1983.5, A.min, 1.0 / 128, A.mult)
+    def ring(out, t, a=0, b=32):
+        ts(out, R(ST[t], 2 * a + 1, 2 * b, 2), 1983.5, A.min, 1.0 / 128, A.mult)
 
     def one_hot(eng="s", a=0, b=32, accum=None):
         out, src = R("eq", 16 * a, 16 * b), ("ind", R("id16"), R("k16", a, b))
@@ -228,39 +234,41 @@ def rank_program(g, core, T, topo):
         else:
             cp(out, src)
 
-    def make_hash(st, t, h):
-        halves = [(0, 128), (128, 256)]
-        for a, b in halves:
-            tt(R("w0", a, b), ("ind", R(st, 64, 128), R("bc", 0, 8)), R("cts", 256 * t + a, 256 * t + b), A.add)
-        for a, b in halves:
-            ts(R("w", a, b), R("w0", a, b), 4095, A.bitwise_and)
-        for a, b in halves:
-            ts(R("pze", a, b), R("w", a, b), 128.0, A.add)
-        for a, b in halves:
-            tt(R("pw", a, b), R("w", a, b), R("pze", a, b), A.mult)
-        for a, b in halves:
-            ts(R(h, a, b), R("pw", a, b), 7, A.logical_shift_right, 4095, A.bitwise_and)
+    def make_hash(st, t, h, after={}):
+        stages = [
+            lambda a, b: tt(R("w0", a, b), ("ind", R(st, 64, 128), R("bc", 0, 8)), R("cts", 256 * t + a, 256 * t + b), A.add),
+            lambda a, b: ts(R("w", a, b), R("w0", a, b), 4095, A.bitwise_and),
+            lambda a, b: ts(R("pze", a, b), R("w", a, b), 128.0, A.add),
+            lambda a, b: tt(R("pw", a, b), R("w", a, b), R("pze", a, b), A.mult),
+            lambda a, b: ts(R(h, a, b), R("pw", a, b), 7, A.logical_shift_right, 4095, A.bitwise_and)]
+        for k in range(2 * len(stages)):
+            stages[k // 2](128 * (k % 2), 128 * (k % 2) + 128)
+            if k in after:
+                after[k]()
 
-    def fallback_wide(x, mv, buf, lo):
+    def fallback_wide(x, mv, buf, lo, between=None):
         mm(R("pzw"), R("ident"), x, True, False)
         mm(R("pzw"), R("nident"), mv, False, True)
         act(R(buf, lo, lo + C), R("pzw"), F.Abs)
+        if between:
+            between()
         act(R(buf, lo + C, lo + 2 * C), R(buf, lo, lo + C), F.Abs, bias=TG[1], scale=-1.0)
 
     def ring_weights(t):
         act(R("zn"), R("zq"), F.Identity, scale=R("nl%d" % t, 0, 1))
 
-    def ring_counts():
-        compact(R("pp", 0, 32), "zn", "eq", 0, C, True, True)
+    def ring_counts(copies):
+        compact(R("pp", 0, 32 * copies), "zn", "eq", 0, C * copies, True, True)
 
     def ring_columns():
         mm(R("po", 0, 256), R("zero"), R("tie"), True, False)
         for i in range(NT):
             mm(R("po", 32 * i, 32 * i + 32), R("ident"), R("kb"), False, False)
 
-    def try_places(h, between=None):
-        for i in range(NT):
-            tt(R("prod", 32 * i, 32 * i + 32), R(h, 32 * i, 32 * i + 32), R("pp", 0, 32), A.mult)
+    def try_places(h, copies, between=None):
+        n = 32 * copies
+        for a in range(0, 256, n):
+            tt(R("prod", a, a + n), R(h, a, a + n), R("pp", 0, n), A.mult)
         for a in (0, 128):
             ts(R("plh", a, a + 128), R("prod", a, a + 128), 1280.0 - 2047.5 / 4096, A.add)
         mm(R("po", 0, 256), R("i16h"), R("plh"), False, True)
@@ -270,7 +278,7 @@ def rank_program(g, core, T, topo):
 
     def open_keys(t):
         mm(R("pw2"), R("ident"), R("W", XO[t], XO[t] + C), True, True)
-        for pk, i in (("pka", 0), ("pes", 4)):
+        for pk, i in (("pka", 0), ("pes", 2)):
             mm(R(pk, 0, 64), R("ident"), R("tie", 32 * i, 32 * i + 64), True, False)
             mm(R(pk, 0, 32), R("ixf"), odd(ST[t], 64), False, False)
             mm(R(pk, 32, 64), R("ixf"), odd(ST[t], 64), False, False)
@@ -302,15 +310,16 @@ def rank_program(g, core, T, topo):
     send(-1, HIST[0], R("W", RB, RB + 16 * M), "ah")
     order("y", [R("st0")], [])
     load("y", "lmv", R("mv", C, 3 * C), T.dv[:, C:3 * C])
-    ring(R("k16"), 0)
-    one_hot()
-    ring(R("ki"), 0)
-    cp(R("kb"), R("ki"))
     cp(col(0), R("tcl", 0, 1))
     cp(N_OLD[0], R("tcl", 1, 2))
+    ring(R("k16"), 0)
+    one_hot("s", 0, 18)
+    ring(R("ki"), 0)
+    one_hot("v", 18, 32)
+    cp(R("kb"), R("ki"))
+    ring_counts(1)
     ring_columns()
-    ring_counts()
-    try_places("hl")
+    try_places("hl", 1)
     open_keys(0)
 
     for t in range(NS):
@@ -329,130 +338,260 @@ def rank_program(g, core, T, topo):
         def top(i):
             tt(R("ad", C * i, C * i + C), R("d", C * i, C * i + C), R("pw2"), A.max)
 
-        def low(pk, i, tie=True):
+        def low(pk, i, tie=True, n=2):
             if tie:
-                mm(R(pk, 0, 64), R("ident"), R("tie", 32 * i, 32 * i + 64), True, False)
-            mm(R(pk, 0, 64), R("i16h"), R("plh", 32 * i, 32 * i + 64), False, False)
+                mm(R(pk, 0, 32 * n), R("ident"), R("tie", 32 * i, 32 * (i + n)), True, False)
+            mm(R(pk, 0, 32 * n), R("i16h"), R("plh", 32 * i, 32 * (i + n)), False, False)
 
-        def keys(pk, z, buf, i, stop):
-            compact(R(pk, 0, 64), z, buf, C * i, C * i + 2 * C, False, stop)
-
-        def new_sums():
-            tt(even("sf"), R("pes", 0, 32), odd("sf"), A.subtract)
-            scan(R(st, 64, 128), R("mk"), R("sf"), 0.0, A.mult, A.add)
+        def keys(pk, z, buf, i, stop, n=2):
+            compact(R(pk, 0, 32 * n), z, buf, C * i, C * (i + n), False, stop)
 
         low("pka", 0, tie=False)
-        low("pes", 4, tie=False)
-        low("pkb", 2)
+        low("pes", 2, tie=False)
+        low("pkb", 4)
+        last = t == NS - 1
+        ends = [("po", [(6, 0, 32)]), ("pp", [(7, 0, 32)])] if last else \
+               [("po", [(6, 0, JA), (7, 0, JA)]), ("pp", [(6, JA, 32), (7, JA, 32)])]
+        spot, at = {}, 32 * 6
+        for bank, pieces in ends:
+            first = at
+            for i, a, b in pieces:
+                spot[i, a] = at
+                at += b - a
+            tie = R("tie", first, at) if last else R("tie2", first - 192, at - 192)
+            mm(R(bank, 0, at - first), R("ident"), tie, True, False)
+            for i, a, b in pieces:
+                mm(R(bank, spot[i, a] - first, spot[i, a] - first + b - a), R("i16h"), R("plh", 32 * i + a, 32 * i + b),
+                   False, False)
+
+        def end_sub(i, a, b, at):
+            tt(R("d", 16 * at, 16 * (at + b - a)), ("ind", HIST[t], R("off", 32 * i + a, 32 * i + b)),
+               R("W", x0 + 16 * a, x0 + 16 * b), A.subtract)
+
+        def end_mag(lo, hi):
+            act(R("ad", 16 * lo, 16 * hi), R("d", 16 * lo, 16 * hi), F.Abs)
+
+        def end_keys(bank, lo, hi):
+            compact(R(bank, 0, hi - lo), "zd", "ad", 16 * lo, 16 * hi, False, True)
+
+        def column(a, b, bank, n):
+            for k in range(n):
+                yield lambda k=k: tt(R("best" if k == n - 1 else "run2", a, b), R("run2", a, b),
+                                     R(bank, k * (b - a), (k + 1) * (b - a)), A.max)
+            yield lambda: ts(R("wp", a, b), R("best", a, b), 0xFF0, A.bitwise_and)
+            yield lambda: tt(R("wc", a, b), R("wp", a, b), R("kb", a, b), A.add)
+            yield lambda: cp(R("w16", a, b), R("wc", a, b))
+
+        bound = [
+            lambda: cp(R("si"), odd(st, 64)),
+            lambda: tt(even(st), R(FZ[t], 32, 64), odd(st), A.subtract),
+            lambda: ts(R("sm"), R("si"), 63, A.bitwise_and),
+            lambda: ts(R("bnd"), R("sm"), TE[t], A.mult),
+            lambda: tt(odd("mk"), even(st), R("bnd"), A.is_le),
+            lambda: tt(R("tm"), R("bnd"), odd(st), A.add),
+            lambda: scan(R("cf"), R("mk"), R("ck", 64 * t, 64 * t + 64), 0.0, A.mult, A.add),
+            lambda: scan(R("ef"), R("mk"), R(st, 0, 64), 0.0, A.mult, A.add)]
+        if t == 0:
+            bound += [lambda: tt(even(st, 64), R(FZ[t], 0, 32), odd(st, 64), A.subtract),
+                      lambda: scan(R("sf"), R("mk"), R(st, 64, 128), 0.0, A.mult, A.add)]
+
+        def mix(*lists):
+            lists = [list(x) for x in lists]
+            while any(lists):
+                for x in lists:
+                    if x:
+                        x.pop(0)()
+
         take(0)
+        sub(4)
         take(1)
-        sub(2)
-        sub(3)
-        keys("pka", "zy", "d", 0, False)
-        mag(2)
-        take(4)
-        mag(3)
         top(0)
+        sub(5)
+        keys("pka", "zy", "d", 0, False)
+        take(2)
         top(1)
         keys("pka", "zm", "ad", 0, True)
-        keys("pkb", "zd", "ad", 2, True)
-        sub(6)
-        take(5)
-        mag(6)
-        top(4)
-        cp(R("run"), R("pka", 0, 64))
-        keys("pes", "zy", "d", 4, False)
-        sub(7, 0, 16)
-        tt(R("run2"), R("run"), R("pkb", 0, 64), A.max)
-        top(5)
-        keys("pes", "zm", "ad", 4, True)
-        low("pkb", 6)
-        sub(7, 16, 32)
-        mag(7, 0, 16)
-        mag(7, 16, 32)
-        keys("pkb", "zd", "ad", 6, True)
-        cp(R("si"), odd(st, 64))
-        tt(even(st, 64), R(FZ[t], 0, 32), odd(st, 64), A.subtract)
-        ts(R("sm"), R("si"), 63, A.bitwise_and)
-        tt(R("tm"), R(FZ[t], 32, 64), odd(st), A.subtract)
-        ts(R("bnd"), R("sm"), TE[t], A.mult)
-        cp(even(st), R("tm"))
-        tt(odd("mk"), R("tm"), R("bnd"), A.is_le)
-        tt(R("tm"), R("bnd"), odd(st), A.add)
-        scan(R("cf"), R("mk"), R("ck", 64 * t, 64 * t + 64), 0.0, A.mult, A.add)
-        scan(R("ef"), R("mk"), R(st, 0, 64), 0.0, A.mult, A.add)
-        scan(R("sf"), R("mk"), R(st, 64, 128), 0.0, A.mult, A.add)
-        tt(R("run"), R("run2"), R("pes", 0, 64), A.max)
-        tt(R("run2"), R("run"), R("pkb", 0, 64), A.max)
-        tt(R("best"), R("run2", 0, 32), R("run2", 32, 64), A.max)
-        ts(R("wp"), R("best"), 0xFF0, A.bitwise_and)
-        tt(R("wc"), R("wp"), R("kb"), A.add)
-        cp(R("w16"), R("wc"))
-        act(R("yb", C, 2 * C), ("ind", HIST[t], R("w16")), F.Abs, bias=TG[t], scale=-1.0)
-        cp(R("yb", 0, C), ("ind", HIST[t], R("w16")))
-        tt(even("cf"), R("wc"), odd("cf"), A.subtract)
-        sums("pes", "yb", 0)
-        tt(odd("mk"), R("pes", 32, 64), R("tm"), A.is_le)
-        tt(even("ef"), R("pes", 32, 64), odd("ef"), A.subtract)
-        last = t == NS - 1
-        xn = [R("xn0"), R("W", XO[2], XO[2] + C), R("xout")][t]
-        picked = ("ind", R("W", XO[t], HB[t] + HN[t]), R("c16"))
+        take(3)
+        top(2)
+        keys("pes", "zy", "d", 2, False)
+        mag(4)
+        top(3)
+        keys("pes", "zm", "ad", 2, True)
+        mag(5)
+        xn = [("xn0", 0), ("W", XO[2]), ("xout", 0)][t]
+        window = R("W", XO[t], HB[t] + HN[t])
+        first_six = [lambda: cp(R("run"), R("pka", 0, 64)),
+                     lambda: tt(R("run2"), R("run"), R("pes", 0, 64), A.max),
+                     lambda: tt(R("run"), R("run2"), R("pkb", 0, 64), A.max),
+                     lambda: tt(R("run2", 0, 32), R("run", 0, 32), R("run", 32, 64), A.max)]
         if last:
+            sub(6)
+            keys("pkb", "zd", "ad", 4, True)
+            first_six[0]()
+            mag(6)
+            sub(7, 0, 20)
+            end_keys("po", 192, 224)
+            first_six[1]()
+            sub(7, 20, 32)
+            mag(7, 0, 20)
+            mag(7, 20, 32)
+            end_keys("pp", 224, 256)
+            mix(bound, first_six[2:] + [lambda: None, lambda: tt(R("run2", 0, 32), R("run2", 0, 32), R("po", 0, 32), A.max)])
+            mix(column(0, 32, "pp", 1))
+        else:
+            mid = 192 + 2 * JA
+            end_sub(6, 0, JA, spot[6, 0])
+            keys("pkb", "zd", "ad", 4, True)
+            end_sub(7, 0, JA, spot[7, 0])
+            first_six[0]()
+            end_mag(192, mid)
+            end_keys("po", 192, mid)
+            end_sub(6, JA, 32, spot[6, JA])
+            first_six[1]()
+            end_mag(mid, spot[7, JA])
+            end_sub(7, JA, 32, spot[7, JA])
+            end_mag(spot[7, JA], 256)
+            end_keys("pp", mid, 256)
+            mix(first_six[2:], bound[:2])
+        if last:
+            act(R("yb", 0, C), ("ind", HIST[t], R("w16")), F.Abs, bias=TG[t], scale=-1.0)
+            tt(even("cf"), R("wc"), odd("cf"), A.subtract)
+            mm(R("pes", 0, 32), R("ident"), R("ce", 32, 64), True, False)
+            compact(R("pes", 0, 32), "z1", "yb", 0, C, False, True)
+            tt(odd("mk"), R("pes", 0, 32), R("tm"), A.is_le)
+            tt(even("ef"), R("pes", 0, 32), odd("ef"), A.subtract)
             scan(R("co"), R("mk"), R("cf"), 0.0, A.mult, A.add)
             scan(R(st, 0, 64), R("mk"), R("ef"), 0.0, A.mult, A.add)
             ts(R("c16"), odd("co"), float(HB[t] - XO[t]), A.add)
             ring(R("k16"), t)
             one_hot(accum=R("cnt", 0, 1))
-            cp(xn, picked)
-            store("y", "sx", T.yx[:], xn)
+            cp(R("xout"), ("ind", window, R("c16")))
+            store("y", "sx", T.yx[:], R("xout"))
             ts(N_NEW[t], R("cnt", 0, 1), N_OLD[t], A.add, 256.0, A.min)
             store("s", "sn", T.yn[:], N_NEW[t])
             break
-        scan(R(st, 0, 64), R("mk"), R("ef"), 0.0, A.mult, A.add)
-        scan(R("co"), R("mk"), R("cf"), 0.0, A.mult, A.add)
-        ring(R("k16"), t)
-        one_hot("s", 0, 18)
-        ts(R("c16"), odd("co"), float(HB[t] - XO[t]), A.add)
-        one_hot("v", 18, 32)
-        act(xn, picked, F.Copy)
-        s, to = str(t + 1), -2 if t == 0 else -1
-        if t == 0:
-            new_sums()
-            send(-1, R("st0"), R("st1"), "ast")
-        else:
-            ring(R("ki"), t)
-        mm(R("pzw"), R("ident"), R("eq"), True, True)
-        scan(R("u"), R("eq"), R("eq"), N_OLD[t], A.add, A.max)
-        if t == 0:
-            ring(R("ki"), t)
+        s, to, x1 = str(t + 1), -2 if t == 0 else -1, XO[t + 1]
+        parts = {"a": (0, JA, "pes", "pzw", "pp"), "b": (JA, 32, "pka", "eq", "pw2")}
+
+        def pair(name, e, lo=0, k=None):
+            a, b = parts[e][:2]
+            return R(name, lo + 2 * a, lo + 2 * b) if k is None else R(name, lo + 2 * a + k, lo + 2 * b, 2)
+
+        def wide(name, e, lo=0):
+            return R(name, lo + 16 * parts[e][0], lo + 16 * parts[e][1])
+
+        def winner(e):
+            a, b, bank = parts[e][:3]
+            extra = 32 if t == 0 and e == "b" else 0
+            lo, n = (a if e == "a" else a + 32) - extra, b - a + extra
+            src = ("ind", HIST[t], R("w16", a, b))
+            act(wide("yb", e, 0 if e == "a" else C), src, F.Abs, bias=TG[t], scale=-1.0)
+            if t == 0:
+                cp(wide("yb", e, 16 * JA), src)
+            mm(R(bank, 0, n), R("ident"), R("ce", 32 - extra, 32 - extra + n), True, False)
+            compact(R(bank, 0, n), "z1", "yb", 16 * lo, 16 * (lo + n), False, True)
+
+        def accept(e):
+            a, b, bank = parts[e][:3]
+            extra = 32 if t == 0 and e == "b" else 0
+            energy = R(bank, extra, extra + b - a)
+            tt(pair("mk", e, 0, 1), energy, R("tm", a, b), A.is_le)
+            tt(pair("ef", e, 0, 0), energy, pair("ef", e, 0, 1), A.subtract)
+            if extra:
+                tt(even("sf"), R(bank, 0, 32), odd("sf"), A.subtract)
+            scan(pair(st, e), pair("mk", e), pair("ef", e), 0.0, A.mult, A.add)
+            if extra:
+                scan(R(st, 64, 128), R("mk"), R("sf"), 0.0, A.mult, A.add)
+                send(-1, R("st0"), R("st1"), "ast")
+            else:
+                scan(pair("co", e), pair("mk", e), pair("cf", e), 0.0, A.mult, A.add)
+            ring(R("k16", a, b), t, a, b)
+            if extra:
+                scan(pair("co", e), pair("mk", e), pair("cf", e), 0.0, A.mult, A.add)
+                ring(R("ki", a, b), t, a, b)
+            ts(R("c16", a, b), pair("co", e, 0, 1), float(HB[t] - XO[t]), A.add)
+
+        def new_state(e):
+            a, b = parts[e][:2]
+            act(wide(xn[0], e, xn[1]), ("ind", window, R("c16", a, b)), F.Copy)
+
+        def running(e, init):
+            if parts[e][3] != "eq":
+                mm(wide(parts[e][3], e), R("ident"), wide("eq", e), True, True)
+            scan(wide("u", e), wide("eq", e), wide("eq", e), init, A.add, A.max)
+
+        def places(e):
+            a, b, _, hot, bank = parts[e]
+            tt(wide("m", e), wide("u", e), wide(hot, e), A.mult)
+            mm(R(bank, a, b), R("ident"), R("kb", a, b), True, False)
+            compact(R(bank, a, b), "z16h", "m", 16 * a, 16 * b, False, True)
+
+        def columns(e):
+            a, b, _, _, bank = parts[e]
+            ts(R("os" + s + e, 0, b - a), R(bank, a, b), -16.0, A.add)
+            send(to, R("os" + s + e, 0, b - a), R("ol" + s + e, 0, b - a), "ao" + s + e)
+
+        def states(e):
+            send(to, wide(xn[0], e, xn[1]), wide("xl" + s, e), "ax" + s + e)
+
+        def enter(e):
+            a, b = parts[e][:2]
+            cp(("ind", R("W", RB, RB + 12288), R("ol" + s + e, 0, b - a)), wide("xl" + s, e))
+
+        column_a, column_b = list(column(0, JA, "po", 2)), list(column(JA, 32, "pp", 2))
+        mix(column_a[:LEAD], bound[2:2 + LEAD])
+        mix(column_a[LEAD:] + [lambda: winner("a")], column_b, bound[2 + LEAD:])
+        winner("b")
+        tt(even("cf"), R("wc"), odd("cf"), A.subtract)
+        accept("a")
+        one_hot("s", 0, JA)
+        new_state("a")
+        ring(R("ki", 0, JA), t, 0, JA)
+        cp(R("kb", 0, JA), R("ki", 0, JA))
+        accept("b")
+        one_hot("s", JA, 32)
+        states("a")
+        running("a", N_OLD[t])
+        if t == 1:
+            ring(R("ki", JA, 32), t, JA, 32)
+        cp(R("cnt", 0, 1), R("u", 16 * JA - 1, 16 * JA))
+        places("a")
+        cp(R("kb", JA, 32), R("ki", JA, 32))
+        new_state("b")
+        running("b", R("cnt", 0, 1))
         ts(N_NEW[t], R("u", C - 1, C), 256.0, A.min)
         send(to, N_NEW[t], R("nl" + s, 0, 1), "an" + s)
-        tt(R("m"), R("u"), R("pzw"), A.mult)
-        cp(R("kb"), R("ki"))
-        send(to, xn, R("xl" + s), "ax" + s)
-        if t == 0:
-            send(-1, xn, R("W", XO[1], XO[1] + C), "axh")
-        compact(R("pp", 0, 32), "z16h", "m", 0, C, True, False)
-        mm(R("pp", 0, 32), R("ident"), R("kb"), False, True)
-        x1 = XO[t + 1]
+        columns("a")
         if t == 1:
-            new_sums()
-            fallback_wide(xn, R("mv", 2 * C, 3 * C), "W", x1 + C)
-        ts(R("os" + s), R("pp", 0, 32), -16.0, A.add)
-        send(to, R("os" + s), R("ol" + s), "ao" + s)
+            compact(R("pkb", 0, 32), "z1", "W", x1, x1 + C, True, True)
+        places("b")
+        if t == 1:
+            cp(odd(st, 64), R("pkb", 0, 32))
+        whole = R(xn[0], xn[1], xn[1] + C)
+        states("b")
         if t == 0:
+            send(-1, whole, R("W", x1, x1 + C), "axh")
+            columns("b")
             send(-1, N_NEW[0], N_OLD[1], "anh")
             ring(R("k16"), 1)
             one_hot()
             ring(R("ki"), 1)
-            cp(R("kb"), R("ki"))
-        make_hash(ST[t + 1], t + 1, "h")
-        ring_columns()
-        ring_weights(t + 1)
-        ring_counts()
-        if t == 0:
+            make_hash(ST[1], 1, "h", {0: lambda: cp(R("kb"), R("ki"))})
+            act(R("eq", C, 2 * C), R("eq", 0, C), F.Copy)
+            ring_weights(1)
+            ring_columns()
+            ring_counts(2)
             fallback_wide(R("W", x1, x1 + C), R("mv", C, 2 * C), "W", x1 + C)
-        try_places("h", lambda: cp(("ind", R("W", RB, RB + 12288), R("ol" + s)), R("xl" + s)))
+            enter("a")
+            try_places("h", 2, lambda: enter("b"))
+        else:
+            act(R("eq", C, 2 * C), R("eq", 0, C), F.Copy)
+            make_hash(ST[2], 2, "h", {1: lambda: columns("b")})
+            fallback_wide(whole, R("mv", 2 * C, 3 * C), "W", x1 + C, lambda: ring_weights(2))
+            ring_columns()
+            ring_counts(2)
+            enter("a")
+            try_places("h", 2, lambda: enter("b"))
         open_keys(t + 1)
         sums("pze", "W", x1 + C)
 

from concourse.mybir import AluOpType as A, ActivationFunctionType as F

C, NT, NS, M = 512, 8, 3, 192
RB = 2 * 1536
XO = [RB + 12288 + 16, 1536, 0]
HB = [XO[0] + 1024, RB, RB]
HN = [16 * M, 4096, 4096]
CH = [(0, 6), (6, 12), (12, 16)]
JA = 16
LEAD = 3
BF, F32, I32, U16, F16 = "bfloat16", "float32", "int32", "uint16", "float16"

SBUF = {
    BF: {"W": HB[0] + HN[0], "hsb": 3072, "xs": 16 + 2048, "mv": 1536, "xn0": 512, "xout": 512, "d": 4096,
         "ad": 4096, "yb": 1024, "eq": 1024, "ident": 128, "nident": 128, "zero": 128, "id16": 16,
         "z1": 144, "zd": 144, "zm": 144, "zy": 144, "zq": 144, "zn": 144, "ce": 64, "tie": 256, "tie2": 64, "kb": 32,
         "xl1": 512, "xl2": 512},
    F32: {"col": 16, "ixf": 128, "cts": 768, "cj": 32, "ck": 192, "mk": 64, "sto": 128, "st0": 128, "st1": 128,
          "fz": 64, "fzl": 64, "co": 64,
          "ef": 64, "sf": 64, "cf": 64, "tm": 32, "bnd": 32, "prod": 256, "run": 64, "run2": 64, "wc": 32, "cnt": 8,
          "na0": 8, "na1": 8, "n1": 8, "n2": 8, "n3": 8, "nl0": 8, "nl1": 8, "nl2": 8},
    I32: {"tc": 8, "tcl": 8, "ia": 128, "ib": 32, "ct": 256, "ki": 32, "si": 32, "sm": 32, "w0": 256, "w": 256, "pw": 256,
          "h": 256, "ho": 256, "hl": 256, "best": 32, "wp": 32},
    U16: {"bc": 16, "k16": 32, "c16": 32, "w16": 32, "off": 256,
          "os1a": 32, "os1b": 32, "os2a": 32, "os2b": 32, "ol1a": 32, "ol1b": 32, "ol2a": 32, "ol2b": 32},
    F16: {"plh": 256, "i16h": 128, "z16h": 144, "u": 512, "m": 512},
}
SCRATCH = {name: ("sbuf", [128, n], dt) for dt, bufs in SBUF.items() for name, n in bufs.items()}
SCRATCH.update({name: ("psum", [128, 512], F32) for name in ("pka", "pkb", "pes", "pzw", "pze", "po", "pp", "pw2")})
LOADS = ["lh%d" % k for k in range(len(CH))] + ["lcn", "lx", "ltg", "lte", "lm0", "lmv", "sx", "sn"]
ARRIVE = ["ax0", "atc", "as0", "ah0", "az0", "af0", "ah", "ast", "axh", "anh", "an1", "an2",
          "ax1a", "ax1b", "ax2a", "ax2b", "ao1a", "ao1b", "ao2a", "ao2b"]
SEMAPHORES = ["qv", "qs", "qp", "qg", "sent"] + LOADS + ARRIVE


def R(name, lo=0, hi=None, step=1):
    return (name, lo, SCRATCH[name][1][1] if hi is None else hi, step)


def rank_program(g, core, T, topo):
    rank = T.rank_of(core)
    if rank is None:
        return
    n_ranks = len(T.cores)
    Q = {"v": g.vector, "s": g.scalar, "p": g.tensor, "g": g, "y": g.sync}
    count = {"qv": 0, "qs": 0, "qp": 0, "qg": 0, "sent": 0}
    known = {q: {} for q in Q}
    log = {name: [] for name in SCRATCH}
    arrivals = {}

    def ap(r):
        return T[r[0]][:, r[1]:r[2]:r[3]] if r[3] != 1 else T[r[0]][:, r[1]:r[2]]

    def cols(r):
        return set(range(r[1], r[2], r[3]))

    def order(q, reads, writes):
        need = {}
        for rs, wr in ((reads, False), (writes, True)):
            for r in rs:
                cs, psum = cols(r), SCRATCH[r[0]][0] == "psum"
                for (c2, w2, q2, sem, val, clock) in log[r[0]]:
                    if q == "p" and q2 == "p":
                        continue
                    clash = (psum and q2 != q) or ((wr or w2) and not cs.isdisjoint(c2))
                    if clash and known[q].get(sem, 0) < val:
                        if val > need.get(sem, (0, None))[0]:
                            need[sem] = (val, clock)
        for sem, (val, clock) in sorted(need.items(), key=lambda e: -sum(e[1][1].values())):
            if known[q].get(sem, 0) < val:
                Q[q].wait_ge(T.sem[sem], val)
                known[q][sem] = val
                for s2, v2 in clock.items():
                    known[q][s2] = max(known[q].get(s2, 0), v2)

    def call(q, make, reads, writes):
        order(q, reads, writes)
        sem = "q" + q
        count[sem] += 1
        make().then_inc(T.sem[sem], 1)
        clock = dict(known[q])
        for r in writes:
            cs = cols(r)
            log[r[0]][:] = [e for e in log[r[0]] if not e[0] <= cs]
            log[r[0]].append((cs, True, q, sem, count[sem], clock))
        for r in reads:
            log[r[0]].append((cols(r), False, q, sem, count[sem], clock))

    def opnd(x):
        if not isinstance(x, tuple):
            return x, [], []
        if x[0] == "ind":
            return ap(x[1]).indirect(ap(x[2])), [x[1]], [x[2]]
        return ap(x), [x], []

    def tt(out, a, b, op):
        (o, wo, _), (x, rx, ox), (y, ry, _) = opnd(out), opnd(a), opnd(b)
        call("v", lambda: g.vector.tensor_tensor(o, x, y, op), rx + ox + ry, wo)

    def ts(out, a, s1, op0, s2=None, op1=None):
        (o, wo, _), (x, rx, ox), (y, ry, _), (z, rz, _) = opnd(out), opnd(a), opnd(s1), opnd(s2)
        if op1 is None:
            call("v", lambda: g.vector.tensor_scalar(o, x, y, None, op0), rx + ox + ry, wo)
        else:
            call("v", lambda: g.vector.tensor_scalar(o, x, y, z, op0, op1), rx + ox + ry + rz, wo)

    def cp(out, a):
        (o, wo, oo), (x, rx, ox) = opnd(out), opnd(a)
        call("v", lambda: g.vector.tensor_copy(o, x), rx + ox + oo, wo)

    def fill(out, v):
        call("v", lambda: g.vector.memset(ap(out), v), [], [out])

    def scan(out, d0, d1, init, op0, op1):
        x, rx, _ = opnd(init)
        call("v", lambda: g.vector.tensor_tensor_scan(ap(out), ap(d0), ap(d1), x, op0, op1), [d0, d1] + rx, [out])

    def act(out, a, func, bias=None, scale=None, accum=None):
        x, rx, ox = opnd(a)
        kw, more = {}, []
        for key, val in (("bias", bias), ("scale", scale)):
            if val is not None:
                kw[key], r, _ = opnd(val)
                more += r
        if accum is not None:
            kw["accum_out"] = ap(accum)
        call("s", lambda: g.scalar.activation(ap(out), x, func, **kw), rx + ox + more, [out] + ([accum] if accum else []))

    def mm(out, lhs, rhs, start, stop):
        call("p", lambda: g.tensor.matmul(ap(out), ap(lhs), ap(rhs), start, stop), [lhs, rhs], [out])

    def compact(out, z, buf, lo, hi, start, stop):
        for p in range(16):
            mm(out, R(z, 15 - p, 143 - p), R(buf, lo + p, hi, 16), start and p == 0, stop and p == 15)

    def load(q, sem, out, dram):
        order(q, [], [out])
        Q[q].dma_start(ap(out), dram).then_inc(T.sem[sem], 16)
        log[out[0]].append((cols(out), True, "dma", sem, 16, dict(known[q])))

    def store(q, sem, dram, a):
        order(q, [a], [])
        Q[q].dma_start(dram, ap(a)).then_inc(T.sem[sem], 16)

    def send(step, a, land, sem):
        dst, src = T.cores[(rank + step) % n_ranks], T.cores[(rank - step) % n_ranks]
        rid, pid = topo.addr(dst, core)
        order("g", [a], [])
        g.remote_dma(ap(land), ap(a), T.sem[sem], T.sem.sent, pid, rid, topo.mask(core, dst))
        count["sent"] += len(topo.engines(core, dst))
        arrivals[sem] = len(topo.engines(src, core))
        log[land[0]].append((cols(land), True, "dma", sem, arrivals[sem], {}))

    def col(j):
        return R("col", j, j + 1)

    def odd(name, lo=0):
        return R(name, lo + 1, lo + 64, 2)

    def even(name, lo=0):
        return R(name, lo, lo + 64, 2)

    HIST = [R("W", HB[t], HB[t] + HN[t]) for t in range(NS)]
    TG = [R("W", XO[0] - 1, XO[0]), R("xs", 15, 16), R("xs", 15, 16)]
    ST = ["st0", "st1", "st1"]
    TE = [col(0), col(1), col(1)]
    N_OLD = [R("na0", 0, 1), R("n1", 0, 1), R("n2", 0, 1)]
    N_NEW = [R("na1", 0, 1), R("n2", 0, 1), R("n3", 0, 1)]
    FZ = ["fzl", "pze", "pze"]

    load("s", "lte", R("tc", 0, 1), T.te[:])
    load("s", "lcn", R("tc", 1, 2), T.cn[:])
    load("y", "ltg", R("xs", 15, 16), T.tg[:])
    load("y", "lx", R("xs", 16, 16 + C), T.x0[:])
    load("y", "lm0", R("mv", 0, C), T.dv[:, 0:C])
    for k, (a, b) in enumerate(CH):
        load("y", "lh%d" % k, R("hsb", M * a, M * b), T.hs[:, M * a:M * b])

    call("g", lambda: g.iota(ap(R("ia")), [[-1, 128]], 0, 1), [], [R("ia")])
    call("g", lambda: g.iota(ap(R("ct")), [[97, NT], [80, 32]], 0, 0), [], [R("ct")])
    call("g", lambda: g.iota(ap(R("tie")), [[-4096, NT], [0, 32]], 4096 * (NT - 1) - 20480, 0,
                             allow_small_or_imprecise_dtypes=True), [], [R("tie")])
    send(1, R("tc", 0, 2), R("tcl", 0, 2), "atc")
    send(1, R("xs", 15, 16 + C), R("W", XO[0] - 1, XO[0] + C), "ax0")
    fill(R("z1"), 0.0)
    fill(R("ce", 0, 32), 0.0)
    fill(R("ce", 32, 64), -63.5)
    fill(R("mk"), 0.0)
    fill(R("sto"), 0.0)
    fill(R("zero"), 0.0)
    fill(R("W", RB + 16 * M, RB + 4096), 0.0)
    fill(R("ck", 0, 192, 2), 512.0)
    for a, b, v in ((0, JA, 4096), (JA, 2 * JA, 0), (2 * JA, 32 + JA, 4096), (32 + JA, 64, 0)):
        fill(R("tie2", a, b), v - 20480.0)
    ts(R("ib", 0, 8), R("ia", 0, 128, 16), 4, A.arith_shift_right)
    ts(R("ib", 8, 24), R("ia", 0, 16), 15, A.bitwise_and)
    ts(R("ident"), R("ia"), 0.0, A.is_equal)
    ts(R("z1", 15, 143, 16), R("ib", 0, 8), 0.0, A.is_equal)
    ts(R("id16"), R("ib", 8, 24), 0.0, A.is_equal)
    cp(col(2), R("ib", 8, 9))
    ts(R("nident"), R("ia"), 0.0, A.is_equal, -1.0, A.mult)
    ts(col(3), col(2), 5.0, A.mult)
    ts(col(4), R("ia", 0, 1), 16.0, A.mult, col(2), A.add)
    ts(R("i16h"), R("ia"), 0.0, A.is_equal, 16.0, A.mult)
    ts(R("cj"), R("ia", 0, 32), -16.0, A.mult, col(4), A.add)
    ts(R("zd"), R("z1"), 32768.0, A.mult)
    ts(R("tm", 0, 2), R("cj", 0, 2), 2.0, A.mult, 1.0, A.add)
    ts(R("cts", 0, 256), R("ct"), col(3), A.add)
    ts(R("bc", 0, 16, 2), R("cj", 0, 8), 0.0, A.mult, R("tm", 0, 1), A.add)
    ts(R("bc", 1, 16, 2), R("cj", 0, 8), 0.0, A.mult, R("tm", 1, 2), A.add)
    ts(R("z16h"), R("z1"), 16.0, A.mult)
    ts(R("zm"), R("z1"), 65536.0, A.mult)
    ts(R("zy"), R("z1"), -32768.0, A.mult)
    ts(R("zq"), R("z1"), 1.0 / 4096, A.mult)
    ts(R("ixf"), R("ia"), 0.0, A.is_equal, -32768.0, A.mult)
    for t in range(NS):
        ts(R("ck", 64 * t + 1, 64 * t + 64, 2), R("cj"), float(XO[t] - HB[t]), A.add)
    for t in range(1, NS):
        ts(R("cts", 256 * t, 256 * t + 256), R("cts", 0, 256), 31.0 * t, A.add)
    cp(col(1), R("tc", 0, 1))
    cp(R("nl0", 0, 1), R("tc", 1, 2))

    def sums(ps, buf, lo):
        mm(R(ps, 0, 64), R("ident"), R("ce"), True, False)
        compact(R(ps, 0, 64), "z1", buf, lo, lo + 1024, False, True)

    def ring(out, t, a=0, b=32):
        ts(out, R(ST[t], 2 * a + 1, 2 * b, 2), 1983.5, A.min, 1.0 / 128, A.mult)

    def one_hot(eng="s", a=0, b=32, accum=None):
        out, src = R("eq", 16 * a, 16 * b), ("ind", R("id16"), R("k16", a, b))
        if eng == "s":
            act(out, src, F.Identity, accum=accum)
        else:
            cp(out, src)

    def make_hash(st, t, h, after={}):
        stages = [
            lambda a, b: tt(R("w0", a, b), ("ind", R(st, 64, 128), R("bc", 0, 8)), R("cts", 256 * t + a, 256 * t + b), A.add),
            lambda a, b: ts(R("w", a, b), R("w0", a, b), 4095, A.bitwise_and),
            lambda a, b: ts(R("pze", a, b), R("w", a, b), 128.0, A.add),
            lambda a, b: tt(R("pw", a, b), R("w", a, b), R("pze", a, b), A.mult),
            lambda a, b: ts(R(h, a, b), R("pw", a, b), 7, A.logical_shift_right, 4095, A.bitwise_and)]
        for k in range(2 * len(stages)):
            stages[k // 2](128 * (k % 2), 128 * (k % 2) + 128)
            if k in after:
                after[k]()

    def fallback_wide(x, mv, buf, lo, between=None):
        mm(R("pzw"), R("ident"), x, True, False)
        mm(R("pzw"), R("nident"), mv, False, True)
        act(R(buf, lo, lo + C), R("pzw"), F.Abs)
        if between:
            between()
        act(R(buf, lo + C, lo + 2 * C), R(buf, lo, lo + C), F.Abs, bias=TG[1], scale=-1.0)

    def ring_weights(t):
        act(R("zn"), R("zq"), F.Identity, scale=R("nl%d" % t, 0, 1))

    def ring_counts(copies):
        compact(R("pp", 0, 32 * copies), "zn", "eq", 0, C * copies, True, True)

    def ring_columns():
        mm(R("po", 0, 256), R("zero"), R("tie"), True, False)
        for i in range(NT):
            mm(R("po", 32 * i, 32 * i + 32), R("ident"), R("kb"), False, False)

    def try_places(h, copies, between=None):
        n = 32 * copies
        for a in range(0, 256, n):
            tt(R("prod", a, a + n), R(h, a, a + n), R("pp", 0, n), A.mult)
        for a in (0, 128):
            ts(R("plh", a, a + 128), R("prod", a, a + 128), 1280.0 - 2047.5 / 4096, A.add)
        mm(R("po", 0, 256), R("i16h"), R("plh"), False, True)
        if between:
            between()
        ts(R("off"), R("po", 0, 256), -20480.0, A.add)

    def open_keys(t):
        mm(R("pw2"), R("ident"), R("W", XO[t], XO[t] + C), True, True)
        for pk, i in (("pka", 0), ("pes", 2)):
            mm(R(pk, 0, 64), R("ident"), R("tie", 32 * i, 32 * i + 64), True, False)
            mm(R(pk, 0, 32), R("ixf"), odd(ST[t], 64), False, False)
            mm(R(pk, 32, 64), R("ixf"), odd(ST[t], 64), False, False)

    def relay(q, eng):
        out, a = R("W", HB[0] + q, HB[0] + 16 * M, 16), R("hsb", M * q, M * q + M)
        if eng == "v":
            cp(out, a)
        else:
            act(out, a, F.Copy)

    act(R("xs", 16 + C, 16 + 2 * C), R("xs", 16, 16 + C), F.Abs, bias=TG[1], scale=-1.0)
    sums("pes", "xs", 16)
    ring_weights(0)
    cp(odd("sto"), R("pes", 32, 64))
    cp(odd("sto", 64), R("pes", 0, 32))
    send(1, R("sto"), R("st0"), "as0")
    for q in range(*CH[0]):
        relay(q, "s")
    make_hash("sto", 0, "ho")
    send(1, R("ho"), R("hl"), "ah0")
    fallback_wide(R("xs", 16, 16 + C), R("mv", 0, C), "xs", 16 + 2 * C)
    send(1, R("xs", 16 + 2 * C, 16 + 3 * C), R("W", XO[0] + C, XO[0] + 2 * C), "az0")
    sums("pze", "xs", 16 + 2 * C)
    for q in range(CH[0][1], 16):
        relay(q, "s" if q % 4 == 1 else "v")
    act(R("fz"), R("pze", 0, 64), F.Copy)
    send(1, R("fz"), R("fzl"), "af0")
    send(-1, HIST[0], R("W", RB, RB + 16 * M), "ah")
    order("y", [R("st0")], [])
    load("y", "lmv", R("mv", C, 3 * C), T.dv[:, C:3 * C])
    cp(col(0), R("tcl", 0, 1))
    cp(N_OLD[0], R("tcl", 1, 2))
    ring(R("k16"), 0)
    one_hot("s", 0, 18)
    ring(R("ki"), 0)
    one_hot("v", 18, 32)
    cp(R("kb"), R("ki"))
    ring_counts(1)
    ring_columns()
    try_places("hl", 1)
    open_keys(0)

    for t in range(NS):
        x0, st = XO[t], ST[t]

        def sub(i, a=0, b=32):
            tt(R("d", C * i + 16 * a, C * i + 16 * b), ("ind", HIST[t], R("off", 32 * i + a, 32 * i + b)),
               R("W", x0 + 16 * a, x0 + 16 * b), A.subtract)

        def mag(i, a=0, b=32):
            act(R("ad", C * i + 16 * a, C * i + 16 * b), R("d", C * i + 16 * a, C * i + 16 * b), F.Abs)

        def take(i):
            act(R("d", C * i, C * i + C), ("ind", HIST[t], R("off", 32 * i, 32 * i + 32)), F.Copy)

        def top(i):
            tt(R("ad", C * i, C * i + C), R("d", C * i, C * i + C), R("pw2"), A.max)

        def low(pk, i, tie=True, n=2):
            if tie:
                mm(R(pk, 0, 32 * n), R("ident"), R("tie", 32 * i, 32 * (i + n)), True, False)
            mm(R(pk, 0, 32 * n), R("i16h"), R("plh", 32 * i, 32 * (i + n)), False, False)

        def keys(pk, z, buf, i, stop, n=2):
            compact(R(pk, 0, 32 * n), z, buf, C * i, C * (i + n), False, stop)

        low("pka", 0, tie=False)
        low("pes", 2, tie=False)
        low("pkb", 4)
        last = t == NS - 1
        ends = [("po", [(6, 0, 32)]), ("pp", [(7, 0, 32)])] if last else \
               [("po", [(6, 0, JA), (7, 0, JA)]), ("pp", [(6, JA, 32), (7, JA, 32)])]
        spot, at = {}, 32 * 6
        for bank, pieces in ends:
            first = at
            for i, a, b in pieces:
                spot[i, a] = at
                at += b - a
            tie = R("tie", first, at) if last else R("tie2", first - 192, at - 192)
            mm(R(bank, 0, at - first), R("ident"), tie, True, False)
            for i, a, b in pieces:
                mm(R(bank, spot[i, a] - first, spot[i, a] - first + b - a), R("i16h"), R("plh", 32 * i + a, 32 * i + b),
                   False, False)

        def end_sub(i, a, b, at):
            tt(R("d", 16 * at, 16 * (at + b - a)), ("ind", HIST[t], R("off", 32 * i + a, 32 * i + b)),
               R("W", x0 + 16 * a, x0 + 16 * b), A.subtract)

        def end_mag(lo, hi):
            act(R("ad", 16 * lo, 16 * hi), R("d", 16 * lo, 16 * hi), F.Abs)

        def end_keys(bank, lo, hi):
            compact(R(bank, 0, hi - lo), "zd", "ad", 16 * lo, 16 * hi, False, True)

        def column(a, b, bank, n):
            for k in range(n):
                yield lambda k=k: tt(R("best" if k == n - 1 else "run2", a, b), R("run2", a, b),
                                     R(bank, k * (b - a), (k + 1) * (b - a)), A.max)
            yield lambda: ts(R("wp", a, b), R("best", a, b), 0xFF0, A.bitwise_and)
            yield lambda: tt(R("wc", a, b), R("wp", a, b), R("kb", a, b), A.add)
            yield lambda: cp(R("w16", a, b), R("wc", a, b))

        bound = [
            lambda: cp(R("si"), odd(st, 64)),
            lambda: tt(even(st), R(FZ[t], 32, 64), odd(st), A.subtract),
            lambda: ts(R("sm"), R("si"), 63, A.bitwise_and),
            lambda: ts(R("bnd"), R("sm"), TE[t], A.mult),
            lambda: tt(odd("mk"), even(st), R("bnd"), A.is_le),
            lambda: tt(R("tm"), R("bnd"), odd(st), A.add),
            lambda: scan(R("cf"), R("mk"), R("ck", 64 * t, 64 * t + 64), 0.0, A.mult, A.add),
            lambda: scan(R("ef"), R("mk"), R(st, 0, 64), 0.0, A.mult, A.add)]
        if t == 0:
            bound += [lambda: tt(even(st, 64), R(FZ[t], 0, 32), odd(st, 64), A.subtract),
                      lambda: scan(R("sf"), R("mk"), R(st, 64, 128), 0.0, A.mult, A.add)]

        def mix(*lists):
            lists = [list(x) for x in lists]
            while any(lists):
                for x in lists:
                    if x:
                        x.pop(0)()

        take(0)
        sub(4)
        take(1)
        top(0)
        sub(5)
        keys("pka", "zy", "d", 0, False)
        take(2)
        top(1)
        keys("pka", "zm", "ad", 0, True)
        take(3)
        top(2)
        keys("pes", "zy", "d", 2, False)
        mag(4)
        top(3)
        keys("pes", "zm", "ad", 2, True)
        mag(5)
        xn = [("xn0", 0), ("W", XO[2]), ("xout", 0)][t]
        window = R("W", XO[t], HB[t] + HN[t])
        first_six = [lambda: cp(R("run"), R("pka", 0, 64)),
                     lambda: tt(R("run2"), R("run"), R("pes", 0, 64), A.max),
                     lambda: tt(R("run"), R("run2"), R("pkb", 0, 64), A.max),
                     lambda: tt(R("run2", 0, 32), R("run", 0, 32), R("run", 32, 64), A.max)]
        if last:
            sub(6)
            keys("pkb", "zd", "ad", 4, True)
            first_six[0]()
            mag(6)
            sub(7, 0, 20)
            end_keys("po", 192, 224)
            first_six[1]()
            sub(7, 20, 32)
            mag(7, 0, 20)
            mag(7, 20, 32)
            end_keys("pp", 224, 256)
            mix(bound, first_six[2:] + [lambda: None, lambda: tt(R("run2", 0, 32), R("run2", 0, 32), R("po", 0, 32), A.max)])
            mix(column(0, 32, "pp", 1))
        else:
            mid = 192 + 2 * JA
            end_sub(6, 0, JA, spot[6, 0])
            keys("pkb", "zd", "ad", 4, True)
            end_sub(7, 0, JA, spot[7, 0])
            first_six[0]()
            end_mag(192, mid)
            end_keys("po", 192, mid)
            end_sub(6, JA, 32, spot[6, JA])
            first_six[1]()
            end_mag(mid, spot[7, JA])
            end_sub(7, JA, 32, spot[7, JA])
            end_mag(spot[7, JA], 256)
            end_keys("pp", mid, 256)
            mix(first_six[2:], bound[:2])
        if last:
            act(R("yb", 0, C), ("ind", HIST[t], R("w16")), F.Abs, bias=TG[t], scale=-1.0)
            tt(even("cf"), R("wc"), odd("cf"), A.subtract)
            mm(R("pes", 0, 32), R("ident"), R("ce", 32, 64), True, False)
            compact(R("pes", 0, 32), "z1", "yb", 0, C, False, True)
            tt(odd("mk"), R("pes", 0, 32), R("tm"), A.is_le)
            tt(even("ef"), R("pes", 0, 32), odd("ef"), A.subtract)
            scan(R("co"), R("mk"), R("cf"), 0.0, A.mult, A.add)
            scan(R(st, 0, 64), R("mk"), R("ef"), 0.0, A.mult, A.add)
            ts(R("c16"), odd("co"), float(HB[t] - XO[t]), A.add)
            ring(R("k16"), t)
            one_hot(accum=R("cnt", 0, 1))
            cp(R("xout"), ("ind", window, R("c16")))
            store("y", "sx", T.yx[:], R("xout"))
            ts(N_NEW[t], R("cnt", 0, 1), N_OLD[t], A.add, 256.0, A.min)
            store("s", "sn", T.yn[:], N_NEW[t])
            break
        s, to, x1 = str(t + 1), -2 if t == 0 else -1, XO[t + 1]
        parts = {"a": (0, JA, "pes", "pzw", "pp"), "b": (JA, 32, "pka", "eq", "pw2")}

        def pair(name, e, lo=0, k=None):
            a, b = parts[e][:2]
            return R(name, lo + 2 * a, lo + 2 * b) if k is None else R(name, lo + 2 * a + k, lo + 2 * b, 2)

        def wide(name, e, lo=0):
            return R(name, lo + 16 * parts[e][0], lo + 16 * parts[e][1])

        def winner(e):
            a, b, bank = parts[e][:3]
            extra = 32 if t == 0 and e == "b" else 0
            lo, n = (a if e == "a" else a + 32) - extra, b - a + extra
            src = ("ind", HIST[t], R("w16", a, b))
            act(wide("yb", e, 0 if e == "a" else C), src, F.Abs, bias=TG[t], scale=-1.0)
            if t == 0:
                cp(wide("yb", e, 16 * JA), src)
            mm(R(bank, 0, n), R("ident"), R("ce", 32 - extra, 32 - extra + n), True, False)
            compact(R(bank, 0, n), "z1", "yb", 16 * lo, 16 * (lo + n), False, True)

        def accept(e):
            a, b, bank = parts[e][:3]
            extra = 32 if t == 0 and e == "b" else 0
            energy = R(bank, extra, extra + b - a)
            tt(pair("mk", e, 0, 1), energy, R("tm", a, b), A.is_le)
            tt(pair("ef", e, 0, 0), energy, pair("ef", e, 0, 1), A.subtract)
            if extra:
                tt(even("sf"), R(bank, 0, 32), odd("sf"), A.subtract)
            scan(pair(st, e), pair("mk", e), pair("ef", e), 0.0, A.mult, A.add)
            if extra:
                scan(R(st, 64, 128), R("mk"), R("sf"), 0.0, A.mult, A.add)
                send(-1, R("st0"), R("st1"), "ast")
            else:
                scan(pair("co", e), pair("mk", e), pair("cf", e), 0.0, A.mult, A.add)
            ring(R("k16", a, b), t, a, b)
            if extra:
                scan(pair("co", e), pair("mk", e), pair("cf", e), 0.0, A.mult, A.add)
                ring(R("ki", a, b), t, a, b)
            ts(R("c16", a, b), pair("co", e, 0, 1), float(HB[t] - XO[t]), A.add)

        def new_state(e):
            a, b = parts[e][:2]
            act(wide(xn[0], e, xn[1]), ("ind", window, R("c16", a, b)), F.Copy)

        def running(e, init):
            if parts[e][3] != "eq":
                mm(wide(parts[e][3], e), R("ident"), wide("eq", e), True, True)
            scan(wide("u", e), wide("eq", e), wide("eq", e), init, A.add, A.max)

        def places(e):
            a, b, _, hot, bank = parts[e]
            tt(wide("m", e), wide("u", e), wide(hot, e), A.mult)
            mm(R(bank, a, b), R("ident"), R("kb", a, b), True, False)
            compact(R(bank, a, b), "z16h", "m", 16 * a, 16 * b, False, True)

        def columns(e):
            a, b, _, _, bank = parts[e]
            ts(R("os" + s + e, 0, b - a), R(bank, a, b), -16.0, A.add)
            send(to, R("os" + s + e, 0, b - a), R("ol" + s + e, 0, b - a), "ao" + s + e)

        def states(e):
            send(to, wide(xn[0], e, xn[1]), wide("xl" + s, e), "ax" + s + e)

        def enter(e):
            a, b = parts[e][:2]
            cp(("ind", R("W", RB, RB + 12288), R("ol" + s + e, 0, b - a)), wide("xl" + s, e))

        column_a, column_b = list(column(0, JA, "po", 2)), list(column(JA, 32, "pp", 2))
        mix(column_a[:LEAD], bound[2:2 + LEAD])
        mix(column_a[LEAD:] + [lambda: winner("a")], column_b, bound[2 + LEAD:])
        winner("b")
        tt(even("cf"), R("wc"), odd("cf"), A.subtract)
        accept("a")
        one_hot("s", 0, JA)
        new_state("a")
        ring(R("ki", 0, JA), t, 0, JA)
        cp(R("kb", 0, JA), R("ki", 0, JA))
        accept("b")
        one_hot("s", JA, 32)
        states("a")
        running("a", N_OLD[t])
        if t == 1:
            ring(R("ki", JA, 32), t, JA, 32)
        cp(R("cnt", 0, 1), R("u", 16 * JA - 1, 16 * JA))
        places("a")
        cp(R("kb", JA, 32), R("ki", JA, 32))
        new_state("b")
        running("b", R("cnt", 0, 1))
        ts(N_NEW[t], R("u", C - 1, C), 256.0, A.min)
        send(to, N_NEW[t], R("nl" + s, 0, 1), "an" + s)
        columns("a")
        if t == 1:
            compact(R("pkb", 0, 32), "z1", "W", x1, x1 + C, True, True)
        places("b")
        if t == 1:
            cp(odd(st, 64), R("pkb", 0, 32))
        whole = R(xn[0], xn[1], xn[1] + C)
        states("b")
        if t == 0:
            send(-1, whole, R("W", x1, x1 + C), "axh")
            columns("b")
            send(-1, N_NEW[0], N_OLD[1], "anh")
            ring(R("k16"), 1)
            one_hot()
            ring(R("ki"), 1)
            make_hash(ST[1], 1, "h", {0: lambda: cp(R("kb"), R("ki"))})
            act(R("eq", C, 2 * C), R("eq", 0, C), F.Copy)
            ring_weights(1)
            ring_columns()
            ring_counts(2)
            fallback_wide(R("W", x1, x1 + C), R("mv", C, 2 * C), "W", x1 + C)
            enter("a")
            try_places("h", 2, lambda: enter("b"))
        else:
            act(R("eq", C, 2 * C), R("eq", 0, C), F.Copy)
            make_hash(ST[2], 2, "h", {1: lambda: columns("b")})
            fallback_wide(whole, R("mv", 2 * C, 3 * C), "W", x1 + C, lambda: ring_weights(2))
            ring_columns()
            ring_counts(2)
            enter("a")
            try_places("h", 2, lambda: enter("b"))
        open_keys(t + 1)
        sums("pze", "W", x1 + C)

    for sem in ("qv", "qs", "qp", "qg", "sent"):
        g.wait_ge(T.sem[sem], count[sem])
    for sem in LOADS:
        g.wait_ge(T.sem[sem], 16)
    for sem in ARRIVE:
        g.wait_ge(T.sem[sem], arrivals[sem])
